import numpy as np
import ml_dtypes


def mxq(x, axis, fmt="e4m3"):
    dtype, down = {"e4m3": (ml_dtypes.float8_e4m3fn, 7), "e5m2": (ml_dtypes.float8_e5m2, 14)}[fmt]
    v = np.moveaxis(np.asarray(x, np.float32).astype(ml_dtypes.bfloat16).astype(np.float64), axis, -1)
    blocks = v.reshape(v.shape[:-1] + (-1, 32))
    amax = np.abs(blocks).max(-1, keepdims=True)
    byte = np.maximum(np.where(amax > 0, np.frexp(amax)[1] - 1 + 127, 0) - down, 1)
    scale = np.exp2(byte - 127.0)
    codes = (blocks / scale).astype(np.float32).astype(dtype).astype(np.float64)
    return np.moveaxis((codes * scale).reshape(v.shape), -1, axis)


WIDE = False


def mx_kscale(k):
    if not WIDE:
        return np.ones(k)
    levels = np.array([10, -10, 5, -5, 0])
    if k % 512:
        return np.exp2(np.random.permutation(np.resize(levels, k // 32))).repeat(32)
    a = np.empty((k // 512, 16))
    for p in range(k // 512):
        a[p, :8] = np.random.permutation(np.resize(levels, 8))
        for g in range(8):
            far = levels[np.abs(levels - a[p, g]) >= 10]
            a[p, g + 8] = far[np.random.randint(len(far))]
    return np.exp2(a.ravel()).repeat(32)


def f64(x):
    return np.asarray(x).astype(np.float64)


def striped(idx):
    return np.tile(np.asarray(idx).reshape(-1, 16).T, (8, 1)).astype(np.uint16)


def unstriped(offs):
    return offs[:16].T.reshape(-1).astype(np.int64)


B, N, T, D, NQ = 1, 512, 2048, 512, 128


def setup_inputs():
    n = np.random.standard_normal
    idx = np.random.permutation(T)[:B * N]
    s = mx_kscale(D)[:, None]
    return {
        "qT": (n((B, D, NQ)) * s * (1.00 / np.sqrt(D))).astype(np.float32),
        "kT": (np.clip(np.round(n((D, T)) * 16), -64, 64) / 16 / s).astype(np.float32),
        "rT": (np.clip(np.round(n((D, T)) * 16), -64, 64) / 16 / s).astype(np.float32),
        "ow": (np.random.uniform(0.5, 2.0, (B, NQ, 1))).astype(np.float32),
        "offs": striped(idx),
    }


def reference(qT, kT, rT, ow, offs):
    idx = unstriped(offs)
    pick = lambda x, which: x[:, which].reshape(x.shape[0], B, -1).transpose(1, 0, 2)
    kg = pick(f64(kT), idx)
    rg = pick(f64(rT), idx)
    ug = mxq(kg - rg, 1, "e4m3")
    qq = mxq(f64(qT), 1, "e4m3")
    a = qq.transpose(0, 2, 1) @ ug
    y = a * f64(ow)
    out = np.zeros((B, NQ, T))
    for b in range(B):
        out[b][:, idx[b * N:(b + 1) * N]] = y[b]
    return out

@@ -1,0 +1,95 @@
+from contextlib import ExitStack
+
+import concourse.mybir as mybir
+
+N, T, D, NQ = 512, 2048, 512, 128
+FLOPS = 2 * D * NQ * N
+
+F32 = mybir.dt.float32
+BF16 = mybir.dt.bfloat16
+U32 = mybir.dt.uint32
+U16 = mybir.dt.uint16
+U8 = mybir.dt.uint8
+FP8X4 = mybir.dt.float8_e4m3fn_x4
+COPY = mybir.ActivationFunctionType.Copy
+SUB = mybir.AluOpType.subtract
+
+P = 128
+PACK = 4
+HALVES = 2
+H = N // HALVES
+LIST_ROWS = 16
+
+
+def tile_attend_pre_diffscat_f_topk_kernel(tc, qT, kT, rT, ow, offs, out):
+    nc = tc.nc
+    with ExitStack() as ctx:
+        keep = ctx.enter_context(tc.tile_pool(name="keep", bufs=1))
+        psum = ctx.enter_context(tc.psum_pool(name="psum", bufs=1))
+
+        offsets = keep.tile([P, N // LIST_ROWS], U16, name="offsets")
+        k_planes = kT.rearrange("(p t) c -> t p c", t=PACK)
+        r_planes = rT.rearrange("(p t) c -> t p c", t=PACK)
+        k_win = [keep.tile([P, T], F32, name=f"k_win{t}") for t in range(PACK)]
+        r_win = [keep.tile([P, T], F32, name=f"r_win{t}") for t in range(PACK)]
+        q_raw = keep.tile([P, PACK, NQ], F32, name="q_raw")
+        ow_col = keep.tile([P, 1], F32, name="ow_col")
+
+        nc.sync.dma_start(offsets[:], offs)
+        nc.scalar.dma_start(ow_col[:], ow[0])
+        for t in range(PACK):
+            nc.sync.dma_start(k_win[t][:], k_planes[t])
+            nc.sync.dma_start(r_win[t][:], r_planes[t])
+        nc.sync.dma_start(q_raw[:], qT[0].rearrange("(p t) q -> p t q", t=PACK))
+
+        out_map = keep.tile([P, T], F32, name="out_map")
+        nc.vector.memset(out_map[:], 0.0)
+
+        u_words = [keep.tile([P, H, PACK], BF16, name=f"u_words{h}", align_bytes=64) for h in range(HALVES)]
+        cols = [slice(h * H, (h + 1) * H) for h in range(HALVES)]
+        list_cols = [slice(h * H // LIST_ROWS, (h + 1) * H // LIST_ROWS) for h in range(HALVES)]
+
+        q_words = keep.tile([P, NQ, PACK], BF16, name="q_words", align_bytes=64)
+        q_codes = keep.tile([P, NQ], U32, name="q_codes", align_bytes=64)
+        q_scales = keep.tile([P, NQ], U8, name="q_scales", align_bytes=64)
+
+        for t in range(PACK):
+            last = t == PACK - 1
+            k_got = keep.tile([P, N], F32, name=f"k_got{t}")
+            nc.vector.tensor_copy(k_got[:], k_win[t][:].indirect(offsets[:]))
+            r_got = [keep.tile([P, H], F32, name=f"r_got{t}_{h}") for h in range(HALVES)]
+            for h in range(HALVES):
+                nc.vector.tensor_copy(r_got[h][:], r_win[t][:].indirect(offsets[:, list_cols[h]]))
+            if last:
+                nc.scalar.activation(q_words[:], q_raw[:].rearrange("p t q -> p q t"), COPY)
+            for h in range(HALVES):
+                u_plane = keep.tile([P, H], BF16, name=f"u_plane{t}_{h}")
+                nc.vector.tensor_tensor(u_plane[:], k_got[:, cols[h]], r_got[h][:], SUB)
+                nc.scalar.activation(u_words[h][:, :, t], u_plane[:], COPY)
+
+        nc.vector.quantize_mx(
+            out=q_codes[:].bitcast(FP8X4), scales=q_scales[:], in_=q_words[:].rearrange("p q t -> p (q t)")
+        )
+        ys = []
+        for h in range(HALVES):
+            u_codes = keep.tile([P, H], U32, name=f"u_codes{h}", align_bytes=64)
+            u_scales = keep.tile([P, H], U8, name=f"u_scales{h}", align_bytes=64)
+            nc.vector.quantize_mx(
+                out=u_codes[:].bitcast(FP8X4), scales=u_scales[:], in_=u_words[h][:].rearrange("p i t -> p (i t)")
+            )
+            acc = psum.tile([NQ, H], F32, name=f"acc{h}")
+            nc.tensor.matmul_mx(
+                out=acc[:],
+                lhsT=q_codes[:].bitcast(FP8X4),
+                lhsT_scale=q_scales[:],
+                rhs=u_codes[:].bitcast(FP8X4),
+                rhs_scale=u_scales[:],
+                start=True,
+                stop=True,
+            )
+            y = keep.tile([NQ, H], F32, name=f"y{h}")
+            nc.scalar.activation(y[:], acc[:], COPY, scale=ow_col[:])
+            ys.append(y)
+        for h in range(HALVES):
+            nc.vector.tensor_copy(out_map[:].indirect(offsets[:, list_cols[h]]), ys[h][:])
+        nc.sync.dma_start(out[0], out_map[:])

@@ -19,6 +19,7 @@ PACK = 4
 HALVES = 2
 H = N // HALVES
 LIST_ROWS = 16
+Q = H // 2
 
 
 def tile_attend_pre_diffscat_f_topk_kernel(tc, qT, kT, rT, ow, offs, out):
@@ -35,61 +36,84 @@ def tile_attend_pre_diffscat_f_topk_kernel(tc, qT, kT, rT, ow, offs, out):
         q_raw = keep.tile([P, PACK, NQ], F32, name="q_raw")
         ow_col = keep.tile([P, 1], F32, name="ow_col")
 
-        nc.sync.dma_start(offsets[:], offs)
-        nc.scalar.dma_start(ow_col[:], ow[0])
         for t in range(PACK):
             nc.sync.dma_start(k_win[t][:], k_planes[t])
+            if t == 0:
+                nc.sync.dma_start(offsets[:], offs)
             nc.sync.dma_start(r_win[t][:], r_planes[t])
         nc.sync.dma_start(q_raw[:], qT[0].rearrange("(p t) q -> p t q", t=PACK))
+        nc.sync.dma_start(ow_col[:], ow[0])
 
         out_map = keep.tile([P, T], F32, name="out_map")
         nc.vector.memset(out_map[:], 0.0)
 
-        u_words = [keep.tile([P, H, PACK], BF16, name=f"u_words{h}", align_bytes=64) for h in range(HALVES)]
-        cols = [slice(h * H, (h + 1) * H) for h in range(HALVES)]
+        u_words = keep.tile([P, HALVES, H, PACK], BF16, name="u_words", align_bytes=64)
         list_cols = [slice(h * H // LIST_ROWS, (h + 1) * H // LIST_ROWS) for h in range(HALVES)]
+        first, second = slice(0, Q), slice(Q, H)
 
         q_words = keep.tile([P, NQ, PACK], BF16, name="q_words", align_bytes=64)
         q_codes = keep.tile([P, NQ], U32, name="q_codes", align_bytes=64)
         q_scales = keep.tile([P, NQ], U8, name="q_scales", align_bytes=64)
+        u_codes = keep.tile([P, HALVES, H], U32, name="u_codes", align_bytes=64)
+        u_scales = keep.tile([P, HALVES, H], U8, name="u_scales", align_bytes=64)
+        y = keep.tile([NQ, HALVES, H], F32, name="y")
 
-        for t in range(PACK):
-            last = t == PACK - 1
-            k_got = keep.tile([P, N], F32, name=f"k_got{t}")
-            nc.vector.tensor_copy(k_got[:], k_win[t][:].indirect(offsets[:]))
-            r_got = [keep.tile([P, H], F32, name=f"r_got{t}_{h}") for h in range(HALVES)]
-            for h in range(HALVES):
-                nc.vector.tensor_copy(r_got[h][:], r_win[t][:].indirect(offsets[:, list_cols[h]]))
-            if last:
-                nc.scalar.activation(q_words[:], q_raw[:].rearrange("p t q -> p q t"), COPY)
-            for h in range(HALVES):
-                u_plane = keep.tile([P, H], BF16, name=f"u_plane{t}_{h}")
-                nc.vector.tensor_tensor(u_plane[:], k_got[:, cols[h]], r_got[h][:], SUB)
-                nc.scalar.activation(u_words[h][:, :, t], u_plane[:], COPY)
+        k_got = [keep.tile([P, HALVES, H], F32, name=f"k_got{t}") for t in range(PACK)]
+        r_got = [keep.tile([P, HALVES, H], F32, name=f"r_got{t}") for t in range(PACK)]
+        u_plane = [keep.tile([P, HALVES, Q], BF16, name=f"u_plane{t}") for t in range(PACK)]
 
-        nc.vector.quantize_mx(
-            out=q_codes[:].bitcast(FP8X4), scales=q_scales[:], in_=q_words[:].rearrange("p q t -> p (q t)")
-        )
-        ys = []
-        for h in range(HALVES):
-            u_codes = keep.tile([P, H], U32, name=f"u_codes{h}", align_bytes=64)
-            u_scales = keep.tile([P, H], U8, name=f"u_scales{h}", align_bytes=64)
+        def subtract_via_scalar(t, hs):
+            nc.vector.tensor_tensor(u_plane[t][:, hs, :], k_got[t][:, hs, first], r_got[t][:, hs, first], SUB)
+            nc.scalar.activation(u_words[:, hs, first, t], u_plane[t][:, hs, :], COPY)
+
+        def subtract_in_place(t, hs):
+            nc.vector.tensor_tensor(u_words[:, hs, second, t], k_got[t][:, hs, second], r_got[t][:, hs, second], SUB)
+
+        def quantize(h, cols):
             nc.vector.quantize_mx(
-                out=u_codes[:].bitcast(FP8X4), scales=u_scales[:], in_=u_words[h][:].rearrange("p i t -> p (i t)")
+                out=u_codes[:, h, cols].bitcast(FP8X4),
+                scales=u_scales[:, h, cols],
+                in_=u_words[:, h, cols, :].rearrange("p i t -> p (i t)"),
             )
-            acc = psum.tile([NQ, H], F32, name=f"acc{h}")
+
+        def project(h, cols):
+            acc = psum.tile([NQ, cols.stop - cols.start], F32, name=f"acc{h}_{cols.start}")
             nc.tensor.matmul_mx(
                 out=acc[:],
                 lhsT=q_codes[:].bitcast(FP8X4),
                 lhsT_scale=q_scales[:],
-                rhs=u_codes[:].bitcast(FP8X4),
-                rhs_scale=u_scales[:],
+                rhs=u_codes[:, h, cols].bitcast(FP8X4),
+                rhs_scale=u_scales[:, h, cols],
                 start=True,
                 stop=True,
             )
-            y = keep.tile([NQ, H], F32, name=f"y{h}")
-            nc.scalar.activation(y[:], acc[:], COPY, scale=ow_col[:])
-            ys.append(y)
+            nc.scalar.activation(y[:, h, cols], acc[:], COPY, scale=ow_col[:])
+
+        both = slice(0, HALVES)
+        for t in range(PACK):
+            nc.vector.tensor_copy(k_got[t][:].rearrange("p h i -> p (h i)"), k_win[t][:].indirect(offsets[:]))
+            if t < PACK - 1:
+                nc.vector.tensor_copy(r_got[t][:].rearrange("p h i -> p (h i)"), r_win[t][:].indirect(offsets[:]))
+                subtract_via_scalar(t, both)
+                subtract_in_place(t, both)
+
+        t = PACK - 1
         for h in range(HALVES):
-            nc.vector.tensor_copy(out_map[:].indirect(offsets[:, list_cols[h]]), ys[h][:])
+            nc.vector.tensor_copy(r_got[t][:, h, :], r_win[t][:].indirect(offsets[:, list_cols[h]]))
+        nc.scalar.activation(q_words[:], q_raw[:].rearrange("p t q -> p q t"), COPY)
+        subtract_via_scalar(t, 0)
+        subtract_in_place(t, 0)
+        nc.vector.quantize_mx(
+            out=q_codes[:].bitcast(FP8X4), scales=q_scales[:], in_=q_words[:].rearrange("p q t -> p (q t)")
+        )
+        subtract_via_scalar(t, 1)
+        quantize(0, second)
+        quantize(0, first)
+        subtract_in_place(t, 1)
+        project(0, second)
+        project(0, first)
+        quantize(1, slice(0, H))
+        project(1, slice(0, H))
+        for h in range(HALVES):
+            nc.vector.tensor_copy(out_map[:].indirect(offsets[:, list_cols[h]]), y[:, h, :])
         nc.sync.dma_start(out[0], out_map[:])

@@ -29,18 +29,21 @@ def tile_attend_pre_diffscat_f_topk_kernel(tc, qT, kT, rT, ow, offs, out):
         psum = ctx.enter_context(tc.psum_pool(name="psum", bufs=1))
 
         offsets = keep.tile([P, N // LIST_ROWS], U16, name="offsets")
-        k_planes = kT.rearrange("(p t) c -> t p c", t=PACK)
-        r_planes = rT.rearrange("(p t) c -> t p c", t=PACK)
-        k_win = [keep.tile([P, T], F32, name=f"k_win{t}") for t in range(PACK)]
-        r_win = [keep.tile([P, T], F32, name=f"r_win{t}") for t in range(PACK)]
+        k_planes = kT.rearrange("(p t) c -> p t c", t=PACK)
+        r_planes = rT.rearrange("(p t) c -> p t c", t=PACK)
+        k_pair = keep.tile([P, 2, T], F32, name="k_pair")
+        r_pair = keep.tile([P, 2, T], F32, name="r_pair")
+        k_win = [k_pair[:, 0, :], k_pair[:, 1, :]] + [keep.tile([P, T], F32, name=f"k_win{t}")[:] for t in (2, 3)]
+        r_win = [r_pair[:, 0, :], r_pair[:, 1, :]] + [keep.tile([P, T], F32, name=f"r_win{t}")[:] for t in (2, 3)]
         q_raw = keep.tile([P, PACK, NQ], F32, name="q_raw")
         ow_col = keep.tile([P, 1], F32, name="ow_col")
 
-        for t in range(PACK):
-            nc.sync.dma_start(k_win[t][:], k_planes[t])
-            if t == 0:
-                nc.sync.dma_start(offsets[:], offs)
-            nc.sync.dma_start(r_win[t][:], r_planes[t])
+        nc.sync.dma_start(k_pair[:], k_planes[:, 0:2, :])
+        nc.sync.dma_start(offsets[:], offs)
+        nc.sync.dma_start(r_pair[:], r_planes[:, 0:2, :])
+        for t in (2, 3):
+            nc.sync.dma_start(k_win[t], k_planes[:, t, :])
+            nc.sync.dma_start(r_win[t], r_planes[:, t, :])
         nc.sync.dma_start(q_raw[:], qT[0].rearrange("(p t) q -> p t q", t=PACK))
         nc.sync.dma_start(ow_col[:], ow[0])
 
@@ -60,11 +63,11 @@ def tile_attend_pre_diffscat_f_topk_kernel(tc, qT, kT, rT, ow, offs, out):
 
         k_got = [keep.tile([P, HALVES, H], F32, name=f"k_got{t}") for t in range(PACK)]
         r_got = [keep.tile([P, HALVES, H], F32, name=f"r_got{t}") for t in range(PACK)]
-        u_plane = [keep.tile([P, HALVES, Q], BF16, name=f"u_plane{t}") for t in range(PACK)]
+        u_plane = [keep.tile([P, HALVES, H], BF16, name=f"u_plane{t}") for t in range(PACK)]
 
-        def subtract_via_scalar(t, hs):
-            nc.vector.tensor_tensor(u_plane[t][:, hs, :], k_got[t][:, hs, first], r_got[t][:, hs, first], SUB)
-            nc.scalar.activation(u_words[:, hs, first, t], u_plane[t][:, hs, :], COPY)
+        def subtract_via_scalar(t, hs, cols):
+            nc.vector.tensor_tensor(u_plane[t][:, hs, cols], k_got[t][:, hs, cols], r_got[t][:, hs, cols], SUB)
+            nc.scalar.activation(u_words[:, hs, cols, t], u_plane[t][:, hs, cols], COPY)
 
         def subtract_in_place(t, hs):
             nc.vector.tensor_tensor(u_words[:, hs, second, t], k_got[t][:, hs, second], r_got[t][:, hs, second], SUB)
@@ -90,24 +93,33 @@ def tile_attend_pre_diffscat_f_topk_kernel(tc, qT, kT, rT, ow, offs, out):
             nc.scalar.activation(y[:, h, cols], acc[:], COPY, scale=ow_col[:])
 
         both = slice(0, HALVES)
-        for t in range(PACK):
-            nc.vector.tensor_copy(k_got[t][:].rearrange("p h i -> p (h i)"), k_win[t][:].indirect(offsets[:]))
-            if t < PACK - 1:
-                nc.vector.tensor_copy(r_got[t][:].rearrange("p h i -> p (h i)"), r_win[t][:].indirect(offsets[:]))
-                subtract_via_scalar(t, both)
-                subtract_in_place(t, both)
+        def gather(got, win):
+            nc.vector.tensor_copy(got[:].rearrange("p h i -> p (h i)"), win.indirect(offsets[:]))
+
+        for t in (0, 1):
+            gather(k_got[t], k_win[t])
+        for t in (0, 1):
+            gather(r_got[t], r_win[t])
+            subtract_via_scalar(t, both, slice(0, H))
+        gather(k_got[2], k_win[2])
+        gather(r_got[2], r_win[2])
+        subtract_via_scalar(2, both, first)
+        subtract_in_place(2, both)
+        gather(k_got[3], k_win[3])
 
         t = PACK - 1
         for h in range(HALVES):
-            nc.vector.tensor_copy(r_got[t][:, h, :], r_win[t][:].indirect(offsets[:, list_cols[h]]))
-        nc.scalar.activation(q_words[:], q_raw[:].rearrange("p t q -> p q t"), COPY)
-        subtract_via_scalar(t, 0)
+            nc.vector.tensor_copy(r_got[t][:, h, :], r_win[t].indirect(offsets[:, list_cols[h]]))
+        nc.scalar.activation(
+            q_words[:].rearrange("p (c i) t -> p c t i", i=4), q_raw[:].rearrange("p t (c i) -> p c t i", i=4), COPY
+        )
+        subtract_via_scalar(t, 0, first)
         subtract_in_place(t, 0)
         nc.vector.quantize_mx(
             out=q_codes[:].bitcast(FP8X4), scales=q_scales[:], in_=q_words[:].rearrange("p q t -> p (q t)")
         )
-        subtract_via_scalar(t, 1)
         quantize(0, second)
+        subtract_via_scalar(t, 1, first)
         quantize(0, first)
         subtract_in_place(t, 1)
         project(0, second)

@@ -13,13 +13,14 @@ U8 = mybir.dt.uint8
 FP8X4 = mybir.dt.float8_e4m3fn_x4
 COPY = mybir.ActivationFunctionType.Copy
 SUB = mybir.AluOpType.subtract
+ADD = mybir.AluOpType.add
 
 P = 128
 PACK = 4
-HALVES = 2
-H = N // HALVES
 LIST_ROWS = 16
-Q = H // 2
+CHUNK = 128
+CHUNKS = N // CHUNK
+HALF = N // 2
 
 
 def tile_attend_pre_diffscat_f_topk_kernel(tc, qT, kT, rT, ow, offs, out):
@@ -31,16 +32,16 @@ def tile_attend_pre_diffscat_f_topk_kernel(tc, qT, kT, rT, ow, offs, out):
         offsets = keep.tile([P, N // LIST_ROWS], U16, name="offsets")
         k_planes = kT.rearrange("(p t) c -> p t c", t=PACK)
         r_planes = rT.rearrange("(p t) c -> p t c", t=PACK)
-        k_pair = keep.tile([P, 2, T], F32, name="k_pair")
-        r_pair = keep.tile([P, 2, T], F32, name="r_pair")
-        k_win = [k_pair[:, 0, :], k_pair[:, 1, :]] + [keep.tile([P, T], F32, name=f"k_win{t}")[:] for t in (2, 3)]
-        r_win = [r_pair[:, 0, :], r_pair[:, 1, :]] + [keep.tile([P, T], F32, name=f"r_win{t}")[:] for t in (2, 3)]
-        q_raw = keep.tile([P, PACK, NQ], F32, name="q_raw")
+        k_head = keep.tile([P, 2, T], F32, name="k_head")
+        r_head = keep.tile([P, 2, T], F32, name="r_head")
+        k_win = [k_head[:, 0, :], k_head[:, 1, :]] + [keep.tile([P, T], F32, name=f"k_win{t}")[:] for t in (2, 3)]
+        r_win = [r_head[:, 0, :], r_head[:, 1, :]] + [keep.tile([P, T], F32, name=f"r_win{t}")[:] for t in (2, 3)]
+        q_raw = keep.tile([P, PACK, NQ], F32, name="q_raw", tag="after_q", align_bytes=64)
         ow_col = keep.tile([P, 1], F32, name="ow_col")
 
-        nc.sync.dma_start(k_pair[:], k_planes[:, 0:2, :])
+        nc.sync.dma_start(k_head[:], k_planes[:, 0:2, :])
         nc.sync.dma_start(offsets[:], offs)
-        nc.sync.dma_start(r_pair[:], r_planes[:, 0:2, :])
+        nc.sync.dma_start(r_head[:], r_planes[:, 0:2, :])
         for t in (2, 3):
             nc.sync.dma_start(k_win[t], k_planes[:, t, :])
             nc.sync.dma_start(r_win[t], r_planes[:, t, :])
@@ -49,83 +50,92 @@ def tile_attend_pre_diffscat_f_topk_kernel(tc, qT, kT, rT, ow, offs, out):
 
         out_map = keep.tile([P, T], F32, name="out_map")
         nc.vector.memset(out_map[:], 0.0)
+        zeros = keep.tile([P, CHUNK], F32, name="zeros")
+        nc.vector.memset(zeros[:], 0.0)
 
-        u_words = keep.tile([P, HALVES, H, PACK], BF16, name="u_words", align_bytes=64)
-        list_cols = [slice(h * H // LIST_ROWS, (h + 1) * H // LIST_ROWS) for h in range(HALVES)]
-        first, second = slice(0, Q), slice(Q, H)
-
+        cols = [slice(c * CHUNK, (c + 1) * CHUNK) for c in range(CHUNKS)]
+        k_got = [keep.tile([P, 2, N], F32, name=f"k_got{w}") for w in range(2)]
+        r_got = [keep.tile([P, 2, N], F32, name=f"r_got{w}") for w in range(2)]
+        u_low = keep.tile([P, 2, N], BF16, name="u_low")
+        u_high = {c: keep.tile([P, 2, CHUNK], BF16, name=f"u_high{c}") for c in (1, 2)}
+        u_words = [keep.tile([P, CHUNK, PACK], BF16, name=f"u_words{c}", align_bytes=64) for c in range(CHUNKS - 1)]
+        u_codes = [keep.tile([P, CHUNK], U32, name=f"u_codes{c}", align_bytes=64) for c in range(CHUNKS)]
+        u_scales = [keep.tile([P, CHUNK], U8, name=f"u_scales{c}", align_bytes=64) for c in range(CHUNKS)]
         q_words = keep.tile([P, NQ, PACK], BF16, name="q_words", align_bytes=64)
         q_codes = keep.tile([P, NQ], U32, name="q_codes", align_bytes=64)
         q_scales = keep.tile([P, NQ], U8, name="q_scales", align_bytes=64)
-        u_codes = keep.tile([P, HALVES, H], U32, name="u_codes", align_bytes=64)
-        u_scales = keep.tile([P, HALVES, H], U8, name="u_scales", align_bytes=64)
-        y = keep.tile([NQ, HALVES, H], F32, name="y")
+        y = keep.tile([NQ, N], F32, name="y")
 
-        k_got = [keep.tile([P, HALVES, H], F32, name=f"k_got{t}") for t in range(PACK)]
-        r_got = [keep.tile([P, HALVES, H], F32, name=f"r_got{t}") for t in range(PACK)]
-        u_plane = [keep.tile([P, HALVES, H], BF16, name=f"u_plane{t}") for t in range(PACK)]
+        def listed(first, last):
+            return offsets[:, first // LIST_ROWS : last // LIST_ROWS]
 
-        def subtract_via_scalar(t, hs, cols):
-            nc.vector.tensor_tensor(u_plane[t][:, hs, cols], k_got[t][:, hs, cols], r_got[t][:, hs, cols], SUB)
-            nc.scalar.activation(u_words[:, hs, cols, t], u_plane[t][:, hs, cols], COPY)
+        def gather(got, win, t, first=0, last=N):
+            nc.vector.tensor_copy(got[t // 2][:, t % 2, first:last], win[t].indirect(listed(first, last)))
 
-        def subtract_in_place(t, hs):
-            nc.vector.tensor_tensor(u_words[:, hs, second, t], k_got[t][:, hs, second], r_got[t][:, hs, second], SUB)
+        def subtract_plane(c, t):
+            nc.vector.tensor_tensor(u_high[c][:, t % 2, :], k_got[1][:, t % 2, cols[c]], r_got[1][:, t % 2, cols[c]], SUB)
 
-        def quantize(h, cols):
-            nc.vector.quantize_mx(
-                out=u_codes[:, h, cols].bitcast(FP8X4),
-                scales=u_scales[:, h, cols],
-                in_=u_words[:, h, cols, :].rearrange("p i t -> p (i t)"),
+        def interleave(c, w, planes):
+            nc.scalar.activation(u_words[c][:, :, 2 * w : 2 * w + 2], planes.rearrange("p t i -> p i t"), COPY)
+
+        def subtract_in_place(c):
+            nc.vector.tensor_tensor(
+                u_words[c][:, :, 2:4],
+                k_got[1][:, :, cols[c]].rearrange("p t i -> p i t"),
+                r_got[1][:, :, cols[c]].rearrange("p t i -> p i t"),
+                SUB,
             )
 
-        def project(h, cols):
-            acc = psum.tile([NQ, cols.stop - cols.start], F32, name=f"acc{h}_{cols.start}")
+        def quantize(codes, scales, words):
+            nc.vector.quantize_mx(
+                out=codes[:].bitcast(FP8X4), scales=scales[:], in_=words[:].rearrange("p i t -> p (i t)")
+            )
+
+        def project(c):
+            quantize(u_codes[c], u_scales[c], u_words[c])
+            acc = psum.tile([NQ, CHUNK], F32, name=f"acc{c}")
             nc.tensor.matmul_mx(
                 out=acc[:],
                 lhsT=q_codes[:].bitcast(FP8X4),
                 lhsT_scale=q_scales[:],
-                rhs=u_codes[:, h, cols].bitcast(FP8X4),
-                rhs_scale=u_scales[:, h, cols],
+                rhs=u_codes[c][:].bitcast(FP8X4),
+                rhs_scale=u_scales[c][:],
                 start=True,
                 stop=True,
             )
-            nc.scalar.activation(y[:, h, cols], acc[:], COPY, scale=ow_col[:])
-
-        both = slice(0, HALVES)
-        def gather(got, win):
-            nc.vector.tensor_copy(got[:].rearrange("p h i -> p (h i)"), win.indirect(offsets[:]))
+            nc.scalar.activation(y[:, cols[c]], acc[:], COPY, scale=ow_col[:])
 
         for t in (0, 1):
-            gather(k_got[t], k_win[t])
+            gather(k_got, k_win, t)
         for t in (0, 1):
-            gather(r_got[t], r_win[t])
-            subtract_via_scalar(t, both, slice(0, H))
-        gather(k_got[2], k_win[2])
-        gather(r_got[2], r_win[2])
-        subtract_via_scalar(2, both, first)
-        subtract_in_place(2, both)
-        gather(k_got[3], k_win[3])
+            gather(r_got, r_win, t)
+        nc.vector.tensor_tensor(u_low[:], k_got[0][:], r_got[0][:], SUB)
+        for c in range(CHUNKS - 1):
+            interleave(c, 0, u_low[:, :, cols[c]])
+        gather(k_got, k_win, 2)
+        gather(r_got, r_win, 2)
+        gather(k_got, k_win, 3)
+        for c in (1, 2):
+            subtract_plane(c, 2)
 
-        t = PACK - 1
-        for h in range(HALVES):
-            nc.vector.tensor_copy(r_got[t][:, h, :], r_win[t].indirect(offsets[:, list_cols[h]]))
+        gather(r_got, r_win, 3, 0, HALF)
+        gather(r_got, r_win, 3, HALF, N)
         nc.scalar.activation(
             q_words[:].rearrange("p (c i) t -> p c t i", i=4), q_raw[:].rearrange("p t (c i) -> p c t i", i=4), COPY
         )
-        subtract_via_scalar(t, 0, first)
-        subtract_in_place(t, 0)
-        nc.vector.quantize_mx(
-            out=q_codes[:].bitcast(FP8X4), scales=q_scales[:], in_=q_words[:].rearrange("p q t -> p (q t)")
-        )
-        quantize(0, second)
-        subtract_via_scalar(t, 1, first)
-        quantize(0, first)
-        subtract_in_place(t, 1)
-        project(0, second)
-        project(0, first)
-        quantize(1, slice(0, H))
-        project(1, slice(0, H))
-        for h in range(HALVES):
-            nc.vector.tensor_copy(out_map[:].indirect(offsets[:, list_cols[h]]), y[:, h, :])
+        subtract_plane(1, 3)
+        interleave(1, 1, u_high[1][:])
+        subtract_in_place(0)
+        subtract_plane(2, 3)
+        interleave(2, 1, u_high[2][:])
+        quantize(q_codes, q_scales, q_words)
+        project(0)
+        project(1)
+        u_words.append(keep.tile([P, CHUNK, PACK], BF16, name="u_words3", tag="after_q", align_bytes=64))
+        subtract_in_place(3)
+        interleave(3, 0, u_low[:, :, cols[3]])
+        project(2)
+        project(3)
+        nc.vector.tensor_tensor(out_map[:].indirect(listed(0, CHUNK)), y[:, 0:CHUNK], zeros[:], ADD)
+        nc.vector.tensor_copy(out_map[:].indirect(listed(CHUNK, N)), y[:, CHUNK:N])
         nc.sync.dma_start(out[0], out_map[:])

@@ -123,6 +123,8 @@ def tile_attend_pre_diffscat_f_topk_kernel(tc, qT, kT, rT, ow, offs, out):
         nc.scalar.activation(
             q_words[:].rearrange("p (c i) t -> p c t i", i=4), q_raw[:].rearrange("p t (c i) -> p c t i", i=4), COPY
         )
+        u_words.append(keep.tile([P, CHUNK, PACK], BF16, name="u_words3", tag="after_q", align_bytes=64))
+        interleave(3, 0, u_low[:, :, cols[3]])
         subtract_plane(1, 3)
         interleave(1, 1, u_high[1][:])
         subtract_in_place(0)
@@ -131,9 +133,7 @@ def tile_attend_pre_diffscat_f_topk_kernel(tc, qT, kT, rT, ow, offs, out):
         quantize(q_codes, q_scales, q_words)
         project(0)
         project(1)
-        u_words.append(keep.tile([P, CHUNK, PACK], BF16, name="u_words3", tag="after_q", align_bytes=64))
         subtract_in_place(3)
-        interleave(3, 0, u_low[:, :, cols[3]])
         project(2)
         project(3)
         nc.vector.tensor_tensor(out_map[:].indirect(listed(0, CHUNK)), y[:, 0:CHUNK], zeros[:], ADD)

@@ -27,6 +27,7 @@ def tile_attend_pre_diffscat_f_topk_kernel(tc, qT, kT, rT, ow, offs, out):
     nc = tc.nc
     with ExitStack() as ctx:
         keep = ctx.enter_context(tc.tile_pool(name="keep", bufs=1))
+        shared = ctx.enter_context(tc.tile_pool(name="shared", bufs=1))
         psum = ctx.enter_context(tc.psum_pool(name="psum", bufs=1))
 
         offsets = keep.tile([P, N // LIST_ROWS], U16, name="offsets")
@@ -36,7 +37,7 @@ def tile_attend_pre_diffscat_f_topk_kernel(tc, qT, kT, rT, ow, offs, out):
         r_head = keep.tile([P, 2, T], F32, name="r_head")
         k_win = [k_head[:, 0, :], k_head[:, 1, :]] + [keep.tile([P, T], F32, name=f"k_win{t}")[:] for t in (2, 3)]
         r_win = [r_head[:, 0, :], r_head[:, 1, :]] + [keep.tile([P, T], F32, name=f"r_win{t}")[:] for t in (2, 3)]
-        q_raw = keep.tile([P, PACK, NQ], F32, name="q_raw", tag="after_q", align_bytes=64)
+        q_raw = shared.tile([P, PACK, NQ], F32, name="q_raw", align_bytes=64, offset=0)
         ow_col = keep.tile([P, 1], F32, name="ow_col")
 
         nc.sync.dma_start(k_head[:], k_planes[:, 0:2, :])
@@ -59,7 +60,7 @@ def tile_attend_pre_diffscat_f_topk_kernel(tc, qT, kT, rT, ow, offs, out):
         u_low = keep.tile([P, 2, N], BF16, name="u_low")
         u_high = {c: keep.tile([P, 2, CHUNK], BF16, name=f"u_high{c}") for c in (1, 2)}
         u_words = [keep.tile([P, CHUNK, PACK], BF16, name=f"u_words{c}", align_bytes=64) for c in range(CHUNKS - 1)]
-        u_codes = [keep.tile([P, CHUNK], U32, name=f"u_codes{c}", align_bytes=64) for c in range(CHUNKS)]
+        u_codes = {c: keep.tile([P, CHUNK], U32, name=f"u_codes{c}", align_bytes=64) for c in range(1, CHUNKS)}
         u_scales = [keep.tile([P, CHUNK], U8, name=f"u_scales{c}", align_bytes=64) for c in range(CHUNKS)]
         q_words = keep.tile([P, NQ, PACK], BF16, name="q_words", align_bytes=64)
         q_codes = keep.tile([P, NQ], U32, name="q_codes", align_bytes=64)
@@ -123,7 +124,8 @@ def tile_attend_pre_diffscat_f_topk_kernel(tc, qT, kT, rT, ow, offs, out):
         nc.scalar.activation(
             q_words[:].rearrange("p (c i) t -> p c t i", i=4), q_raw[:].rearrange("p t (c i) -> p c t i", i=4), COPY
         )
-        u_words.append(keep.tile([P, CHUNK, PACK], BF16, name="u_words3", tag="after_q", align_bytes=64))
+        u_words.append(shared.tile([P, CHUNK, PACK], BF16, name="u_words3", align_bytes=64, offset=0))
+        u_codes[0] = shared.tile([P, CHUNK], U32, name="u_codes0", align_bytes=64, offset=1024)
         interleave(3, 0, u_low[:, :, cols[3]])
         subtract_plane(1, 3)
         interleave(1, 1, u_high[1][:])
@@ -132,8 +134,8 @@ def tile_attend_pre_diffscat_f_topk_kernel(tc, qT, kT, rT, ow, offs, out):
         interleave(2, 1, u_high[2][:])
         quantize(q_codes, q_scales, q_words)
         project(0)
-        project(1)
         subtract_in_place(3)
+        project(1)
         project(2)
         project(3)
         nc.vector.tensor_tensor(out_map[:].indirect(listed(0, CHUNK)), y[:, 0:CHUNK], zeros[:], ADD)

@@ -56,11 +56,10 @@ def tile_attend_pre_diffscat_f_topk_kernel(tc, qT, kT, rT, ow, offs, out):
 
         cols = [slice(c * CHUNK, (c + 1) * CHUNK) for c in range(CHUNKS)]
         k_got = [keep.tile([P, 2, N], F32, name=f"k_got{w}") for w in range(2)]
-        r_got = [keep.tile([P, 2, N], F32, name=f"r_got{w}") for w in range(2)]
-        u_low = keep.tile([P, 2, N], BF16, name="u_low")
-        u_high = {c: keep.tile([P, 2, CHUNK], BF16, name=f"u_high{c}") for c in (1, 2)}
+        r_got = [keep.tile([P, 2, N], F32, name="r_got0"), shared.tile([P, 2, N], F32, name="r_got1", align_bytes=64, offset=2048)]
+        u_low = keep.tile([P, 3, N], BF16, name="u_low")
         u_words = [keep.tile([P, CHUNK, PACK], BF16, name=f"u_words{c}", align_bytes=64) for c in range(CHUNKS - 1)]
-        u_codes = {c: keep.tile([P, CHUNK], U32, name=f"u_codes{c}", align_bytes=64) for c in range(1, CHUNKS)}
+        u_codes = {c: keep.tile([P, CHUNK], U32, name=f"u_codes{c}", align_bytes=64) for c in (1, 3)}
         u_scales = [keep.tile([P, CHUNK], U8, name=f"u_scales{c}", align_bytes=64) for c in range(CHUNKS)]
         q_words = keep.tile([P, NQ, PACK], BF16, name="q_words", align_bytes=64)
         q_codes = keep.tile([P, NQ], U32, name="q_codes", align_bytes=64)
@@ -73,11 +72,13 @@ def tile_attend_pre_diffscat_f_topk_kernel(tc, qT, kT, rT, ow, offs, out):
         def gather(got, win, t, first=0, last=N):
             nc.vector.tensor_copy(got[t // 2][:, t % 2, first:last], win[t].indirect(listed(first, last)))
 
-        def subtract_plane(c, t):
-            nc.vector.tensor_tensor(u_high[c][:, t % 2, :], k_got[1][:, t % 2, cols[c]], r_got[1][:, t % 2, cols[c]], SUB)
+        def subtract_last(c):
+            last = shared.tile([P, CHUNK], BF16, name=f"u_last{c}", align_bytes=64, offset=1280 + 256 * c)
+            nc.vector.tensor_tensor(last[:], k_got[1][:, 1, cols[c]], r_got[1][:, 1, cols[c]], SUB)
+            nc.scalar.activation(u_words[c][:, :, 3], last[:], COPY)
 
-        def interleave(c, w, planes):
-            nc.scalar.activation(u_words[c][:, :, 2 * w : 2 * w + 2], planes.rearrange("p t i -> p i t"), COPY)
+        def interleave(c, planes):
+            nc.scalar.activation(u_words[c][:, :, 0:planes], u_low[:, 0:planes, cols[c]].rearrange("p t i -> p i t"), COPY)
 
         def subtract_in_place(c):
             nc.vector.tensor_tensor(
@@ -110,14 +111,15 @@ def tile_attend_pre_diffscat_f_topk_kernel(tc, qT, kT, rT, ow, offs, out):
             gather(k_got, k_win, t)
         for t in (0, 1):
             gather(r_got, r_win, t)
-        nc.vector.tensor_tensor(u_low[:], k_got[0][:], r_got[0][:], SUB)
-        for c in range(CHUNKS - 1):
-            interleave(c, 0, u_low[:, :, cols[c]])
+        nc.vector.tensor_tensor(u_low[:, 0:2, :], k_got[0][:], r_got[0][:], SUB)
+        interleave(0, 2)
         gather(k_got, k_win, 2)
         gather(r_got, r_win, 2)
-        gather(k_got, k_win, 3)
+        middle = slice(CHUNK, 3 * CHUNK)
+        nc.vector.tensor_tensor(u_low[:, 2, middle], k_got[1][:, 0, middle], r_got[1][:, 0, middle], SUB)
         for c in (1, 2):
-            subtract_plane(c, 2)
+            interleave(c, 3)
+        gather(k_got, k_win, 3)
 
         gather(r_got, r_win, 3, 0, HALF)
         gather(r_got, r_win, 3, HALF, N)
@@ -126,18 +128,17 @@ def tile_attend_pre_diffscat_f_topk_kernel(tc, qT, kT, rT, ow, offs, out):
         )
         u_words.append(shared.tile([P, CHUNK, PACK], BF16, name="u_words3", align_bytes=64, offset=0))
         u_codes[0] = shared.tile([P, CHUNK], U32, name="u_codes0", align_bytes=64, offset=1024)
-        interleave(3, 0, u_low[:, :, cols[3]])
-        subtract_plane(1, 3)
-        interleave(1, 1, u_high[1][:])
+        interleave(3, 2)
         subtract_in_place(0)
-        subtract_plane(2, 3)
-        interleave(2, 1, u_high[2][:])
+        subtract_last(1)
+        subtract_last(2)
         quantize(q_codes, q_scales, q_words)
         project(0)
         subtract_in_place(3)
         project(1)
-        project(2)
         project(3)
+        u_codes[2] = shared.tile([P, CHUNK], U32, name="u_codes2", align_bytes=64, offset=2048)
+        project(2)
         nc.vector.tensor_tensor(out_map[:].indirect(listed(0, CHUNK)), y[:, 0:CHUNK], zeros[:], ADD)
         nc.vector.tensor_copy(out_map[:].indirect(listed(CHUNK, N)), y[:, CHUNK:N])
         nc.sync.dma_start(out[0], out_map[:])

@@ -88,6 +88,9 @@ def tile_attend_pre_diffscat_f_topk_kernel(tc, qT, kT, rT, ow, offs, out):
                 SUB,
             )
 
+        def subtract_plane_in_place(c, t):
+            nc.vector.tensor_tensor(u_words[c][:, :, t], k_got[1][:, t % 2, cols[c]], r_got[1][:, t % 2, cols[c]], SUB)
+
         def quantize(codes, scales, words):
             nc.vector.quantize_mx(
                 out=codes[:].bitcast(FP8X4), scales=scales[:], in_=words[:].rearrange("p i t -> p (i t)")
@@ -119,6 +122,7 @@ def tile_attend_pre_diffscat_f_topk_kernel(tc, qT, kT, rT, ow, offs, out):
         nc.vector.tensor_tensor(u_low[:, 2, middle], k_got[1][:, 0, middle], r_got[1][:, 0, middle], SUB)
         for c in (1, 2):
             interleave(c, 3)
+        subtract_plane_in_place(0, 2)
         gather(k_got, k_win, 3)
 
         gather(r_got, r_win, 3, 0, HALF)
@@ -129,7 +133,7 @@ def tile_attend_pre_diffscat_f_topk_kernel(tc, qT, kT, rT, ow, offs, out):
         u_words.append(shared.tile([P, CHUNK, PACK], BF16, name="u_words3", align_bytes=64, offset=0))
         u_codes[0] = shared.tile([P, CHUNK], U32, name="u_codes0", align_bytes=64, offset=1024)
         interleave(3, 2)
-        subtract_in_place(0)
+        subtract_plane_in_place(0, 3)
         subtract_last(1)
         subtract_last(2)
         quantize(q_codes, q_scales, q_words)

@@ -58,7 +58,7 @@ def tile_attend_pre_diffscat_f_topk_kernel(tc, qT, kT, rT, ow, offs, out):
         k_got = [keep.tile([P, 2, N], F32, name=f"k_got{w}") for w in range(2)]
         r_got = [keep.tile([P, 2, N], F32, name="r_got0"), shared.tile([P, 2, N], F32, name="r_got1", align_bytes=64, offset=2048)]
         u_low = keep.tile([P, 3, N], BF16, name="u_low")
-        u_words = [keep.tile([P, CHUNK, PACK], BF16, name=f"u_words{c}", align_bytes=64) for c in range(CHUNKS - 1)]
+        u_words = [keep.tile([P, CHUNK, PACK], BF16, name=f"u_words{c}", align_bytes=64) for c in range(CHUNKS)]
         u_codes = {c: keep.tile([P, CHUNK], U32, name=f"u_codes{c}", align_bytes=64) for c in (1, 3)}
         u_scales = [keep.tile([P, CHUNK], U8, name=f"u_scales{c}", align_bytes=64) for c in range(CHUNKS)]
         q_words = keep.tile([P, NQ, PACK], BF16, name="q_words", align_bytes=64)
@@ -73,20 +73,12 @@ def tile_attend_pre_diffscat_f_topk_kernel(tc, qT, kT, rT, ow, offs, out):
             nc.vector.tensor_copy(got[t // 2][:, t % 2, first:last], win[t].indirect(listed(first, last)))
 
         def subtract_last(c):
-            last = shared.tile([P, CHUNK], BF16, name=f"u_last{c}", align_bytes=64, offset=1280 + 256 * c)
+            last = keep.tile([P, CHUNK], BF16, name=f"u_last{c}", align_bytes=64)
             nc.vector.tensor_tensor(last[:], k_got[1][:, 1, cols[c]], r_got[1][:, 1, cols[c]], SUB)
             nc.scalar.activation(u_words[c][:, :, 3], last[:], COPY)
 
         def interleave(c, planes):
             nc.scalar.activation(u_words[c][:, :, 0:planes], u_low[:, 0:planes, cols[c]].rearrange("p t i -> p i t"), COPY)
-
-        def subtract_in_place(c):
-            nc.vector.tensor_tensor(
-                u_words[c][:, :, 2:4],
-                k_got[1][:, :, cols[c]].rearrange("p t i -> p i t"),
-                r_got[1][:, :, cols[c]].rearrange("p t i -> p i t"),
-                SUB,
-            )
 
         def subtract_plane_in_place(c, t):
             nc.vector.tensor_tensor(u_words[c][:, :, t], k_got[1][:, t % 2, cols[c]], r_got[1][:, t % 2, cols[c]], SUB)
@@ -116,6 +108,7 @@ def tile_attend_pre_diffscat_f_topk_kernel(tc, qT, kT, rT, ow, offs, out):
             gather(r_got, r_win, t)
         nc.vector.tensor_tensor(u_low[:, 0:2, :], k_got[0][:], r_got[0][:], SUB)
         interleave(0, 2)
+        interleave(3, 2)
         gather(k_got, k_win, 2)
         gather(r_got, r_win, 2)
         middle = slice(CHUNK, 3 * CHUNK)
@@ -123,6 +116,7 @@ def tile_attend_pre_diffscat_f_topk_kernel(tc, qT, kT, rT, ow, offs, out):
         for c in (1, 2):
             interleave(c, 3)
         subtract_plane_in_place(0, 2)
+        subtract_plane_in_place(3, 2)
         gather(k_got, k_win, 3)
 
         gather(r_got, r_win, 3, 0, HALF)
@@ -130,19 +124,19 @@ def tile_attend_pre_diffscat_f_topk_kernel(tc, qT, kT, rT, ow, offs, out):
         nc.scalar.activation(
             q_words[:].rearrange("p (c i) t -> p c t i", i=4), q_raw[:].rearrange("p t (c i) -> p c t i", i=4), COPY
         )
-        u_words.append(shared.tile([P, CHUNK, PACK], BF16, name="u_words3", align_bytes=64, offset=0))
         u_codes[0] = shared.tile([P, CHUNK], U32, name="u_codes0", align_bytes=64, offset=1024)
-        interleave(3, 2)
-        subtract_plane_in_place(0, 3)
         subtract_last(1)
+        subtract_plane_in_place(0, 3)
         subtract_last(2)
         quantize(q_codes, q_scales, q_words)
         project(0)
-        subtract_in_place(3)
+        last3 = shared.tile([P, CHUNK], BF16, name="u_last3", align_bytes=64, offset=0)
+        nc.vector.tensor_tensor(last3[:], k_got[1][:, 1, cols[3]], r_got[1][:, 1, cols[3]], SUB)
         project(1)
-        project(3)
+        nc.vector.tensor_copy(u_words[3][:, :, 3], last3[:])
         u_codes[2] = shared.tile([P, CHUNK], U32, name="u_codes2", align_bytes=64, offset=2048)
         project(2)
+        project(3)
         nc.vector.tensor_tensor(out_map[:].indirect(listed(0, CHUNK)), y[:, 0:CHUNK], zeros[:], ADD)
         nc.vector.tensor_copy(out_map[:].indirect(listed(CHUNK, N)), y[:, CHUNK:N])
         nc.sync.dma_start(out[0], out_map[:])

@@ -75,10 +75,10 @@ def tile_attend_pre_diffscat_f_topk_kernel(tc, qT, kT, rT, ow, offs, out):
         def subtract_last(c):
             last = keep.tile([P, CHUNK], BF16, name=f"u_last{c}", align_bytes=64)
             nc.vector.tensor_tensor(last[:], k_got[1][:, 1, cols[c]], r_got[1][:, 1, cols[c]], SUB)
-            nc.scalar.activation(u_words[c][:, :, 3], last[:], COPY)
+            nc.scalar.copy(u_words[c][:, :, 3], last[:])
 
         def interleave(c, planes):
-            nc.scalar.activation(u_words[c][:, :, 0:planes], u_low[:, 0:planes, cols[c]].rearrange("p t i -> p i t"), COPY)
+            nc.scalar.copy(u_words[c][:, :, 0:planes], u_low[:, 0:planes, cols[c]].rearrange("p t i -> p i t"))
 
         def subtract_plane_in_place(c, t):
             nc.vector.tensor_tensor(u_words[c][:, :, t], k_got[1][:, t % 2, cols[c]], r_got[1][:, t % 2, cols[c]], SUB)
@@ -121,8 +121,8 @@ def tile_attend_pre_diffscat_f_topk_kernel(tc, qT, kT, rT, ow, offs, out):
 
         gather(r_got, r_win, 3, 0, HALF)
         gather(r_got, r_win, 3, HALF, N)
-        nc.scalar.activation(
-            q_words[:].rearrange("p (c i) t -> p c t i", i=4), q_raw[:].rearrange("p t (c i) -> p c t i", i=4), COPY
+        nc.scalar.copy(
+            q_words[:].rearrange("p (c i) t -> p c t i", i=4), q_raw[:].rearrange("p t (c i) -> p c t i", i=4)
         )
         u_codes[0] = shared.tile([P, CHUNK], U32, name="u_codes0", align_bytes=64, offset=1024)
         subtract_last(1)

@@ -33,11 +33,11 @@ def tile_attend_pre_diffscat_f_topk_kernel(tc, qT, kT, rT, ow, offs, out):
         offsets = keep.tile([P, N // LIST_ROWS], U16, name="offsets")
         k_planes = kT.rearrange("(p t) c -> p t c", t=PACK)
         r_planes = rT.rearrange("(p t) c -> p t c", t=PACK)
-        k_head = keep.tile([P, 2, T], F32, name="k_head")
-        r_head = keep.tile([P, 2, T], F32, name="r_head")
-        k_win = [k_head[:, 0, :], k_head[:, 1, :]] + [keep.tile([P, T], F32, name=f"k_win{t}")[:] for t in (2, 3)]
-        r_win = [r_head[:, 0, :], r_head[:, 1, :]] + [keep.tile([P, T], F32, name=f"r_win{t}")[:] for t in (2, 3)]
-        q_raw = shared.tile([P, PACK, NQ], F32, name="q_raw", align_bytes=64, offset=0)
+        k_head = keep.tile([P, 2, T], F32, name="k_head", align_bytes=256)
+        r_head = keep.tile([P, 2, T], F32, name="r_head", align_bytes=256)
+        k_win = [k_head[:, 0, :], k_head[:, 1, :]] + [keep.tile([P, T], F32, name=f"k_win{t}", align_bytes=256)[:] for t in (2, 3)]
+        r_win = [r_head[:, 0, :], r_head[:, 1, :]] + [keep.tile([P, T], F32, name=f"r_win{t}", align_bytes=256)[:] for t in (2, 3)]
+        q_raw = shared.tile([P, PACK, NQ], F32, name="q_raw", align_bytes=256, offset=0)
         ow_col = keep.tile([P, 1], F32, name="ow_col")
 
         nc.sync.dma_start(k_head[:], k_planes[:, 0:2, :])
@@ -49,7 +49,7 @@ def tile_attend_pre_diffscat_f_topk_kernel(tc, qT, kT, rT, ow, offs, out):
         nc.sync.dma_start(q_raw[:], qT[0].rearrange("(p t) q -> p t q", t=PACK))
         nc.sync.dma_start(ow_col[:], ow[0])
 
-        out_map = keep.tile([P, T], F32, name="out_map")
+        out_map = keep.tile([P, T], F32, name="out_map", align_bytes=256)
         nc.vector.memset(out_map[:], 0.0)
         zeros = keep.tile([P, CHUNK], F32, name="zeros")
         nc.vector.memset(zeros[:], 0.0)

@@ -51,20 +51,20 @@ def tile_attend_pre_diffscat_f_topk_kernel(tc, qT, kT, rT, ow, offs, out):
 
         out_map = keep.tile([P, T], F32, name="out_map", align_bytes=256)
         nc.vector.memset(out_map[:], 0.0)
-        zeros = keep.tile([P, CHUNK], F32, name="zeros")
+        zeros = keep.tile([P, CHUNK], F32, name="zeros", align_bytes=256)
         nc.vector.memset(zeros[:], 0.0)
 
         cols = [slice(c * CHUNK, (c + 1) * CHUNK) for c in range(CHUNKS)]
-        k_got = [keep.tile([P, 2, N], F32, name=f"k_got{w}") for w in range(2)]
-        r_got = [keep.tile([P, 2, N], F32, name="r_got0"), shared.tile([P, 2, N], F32, name="r_got1", align_bytes=64, offset=2048)]
-        u_low = keep.tile([P, 3, N], BF16, name="u_low")
-        u_words = [keep.tile([P, CHUNK, PACK], BF16, name=f"u_words{c}", align_bytes=64) for c in range(CHUNKS)]
-        u_codes = {c: keep.tile([P, CHUNK], U32, name=f"u_codes{c}", align_bytes=64) for c in (1, 3)}
-        u_scales = [keep.tile([P, CHUNK], U8, name=f"u_scales{c}", align_bytes=64) for c in range(CHUNKS)]
-        q_words = keep.tile([P, NQ, PACK], BF16, name="q_words", align_bytes=64)
-        q_codes = keep.tile([P, NQ], U32, name="q_codes", align_bytes=64)
-        q_scales = keep.tile([P, NQ], U8, name="q_scales", align_bytes=64)
-        y = keep.tile([NQ, N], F32, name="y")
+        k_got = [keep.tile([P, 2, N], F32, name=f"k_got{w}", align_bytes=256) for w in range(2)]
+        r_got = [keep.tile([P, 2, N], F32, name="r_got0", align_bytes=256), shared.tile([P, 2, N], F32, name="r_got1", align_bytes=256, offset=2048)]
+        u_low = keep.tile([P, 3, N], BF16, name="u_low", align_bytes=256)
+        u_words = [keep.tile([P, CHUNK, PACK], BF16, name=f"u_words{c}", align_bytes=256) for c in range(CHUNKS)]
+        u_codes = {c: keep.tile([P, CHUNK], U32, name=f"u_codes{c}", align_bytes=256) for c in (1, 3)}
+        u_scales = [keep.tile([P, CHUNK], U8, name=f"u_scales{c}", align_bytes=256) for c in range(CHUNKS)]
+        q_words = keep.tile([P, NQ, PACK], BF16, name="q_words", align_bytes=256)
+        q_codes = keep.tile([P, NQ], U32, name="q_codes", align_bytes=256)
+        q_scales = keep.tile([P, NQ], U8, name="q_scales", align_bytes=256)
+        y = keep.tile([NQ, N], F32, name="y", align_bytes=256)
 
         def listed(first, last):
             return offsets[:, first // LIST_ROWS : last // LIST_ROWS]
@@ -73,7 +73,7 @@ def tile_attend_pre_diffscat_f_topk_kernel(tc, qT, kT, rT, ow, offs, out):
             nc.vector.tensor_copy(got[t // 2][:, t % 2, first:last], win[t].indirect(listed(first, last)))
 
         def subtract_last(c):
-            last = keep.tile([P, CHUNK], BF16, name=f"u_last{c}", align_bytes=64)
+            last = keep.tile([P, CHUNK], BF16, name=f"u_last{c}", align_bytes=256)
             nc.vector.tensor_tensor(last[:], k_got[1][:, 1, cols[c]], r_got[1][:, 1, cols[c]], SUB)
             nc.scalar.copy(u_words[c][:, :, 3], last[:])
 
@@ -124,17 +124,17 @@ def tile_attend_pre_diffscat_f_topk_kernel(tc, qT, kT, rT, ow, offs, out):
         nc.scalar.copy(
             q_words[:].rearrange("p (c i) t -> p c t i", i=4), q_raw[:].rearrange("p t (c i) -> p c t i", i=4)
         )
-        u_codes[0] = shared.tile([P, CHUNK], U32, name="u_codes0", align_bytes=64, offset=1024)
+        u_codes[0] = shared.tile([P, CHUNK], U32, name="u_codes0", align_bytes=256, offset=1024)
         subtract_last(1)
         subtract_plane_in_place(0, 3)
         subtract_last(2)
         quantize(q_codes, q_scales, q_words)
         project(0)
-        last3 = shared.tile([P, CHUNK], BF16, name="u_last3", align_bytes=64, offset=0)
+        last3 = shared.tile([P, CHUNK], BF16, name="u_last3", align_bytes=256, offset=0)
         nc.vector.tensor_tensor(last3[:], k_got[1][:, 1, cols[3]], r_got[1][:, 1, cols[3]], SUB)
         project(1)
         nc.vector.tensor_copy(u_words[3][:, :, 3], last3[:])
-        u_codes[2] = shared.tile([P, CHUNK], U32, name="u_codes2", align_bytes=64, offset=2048)
+        u_codes[2] = shared.tile([P, CHUNK], U32, name="u_codes2", align_bytes=256, offset=2048)
         project(2)
         project(3)
         nc.vector.tensor_tensor(out_map[:].indirect(listed(0, CHUNK)), y[:, 0:CHUNK], zeros[:], ADD)

@@ -47,7 +47,8 @@ def tile_attend_pre_diffscat_f_topk_kernel(tc, qT, kT, rT, ow, offs, out):
             nc.sync.dma_start(k_win[t], k_planes[:, t, :])
             nc.sync.dma_start(r_win[t], r_planes[:, t, :])
         nc.sync.dma_start(q_raw[:], qT[0].rearrange("(p t) q -> p t q", t=PACK))
-        nc.sync.dma_start(ow_col[:], ow[0])
+        for first, last in ((0, 32), (32, 64), (64, 80), (80, 96), (96, 112), (112, 128)):
+            nc.sync.dma_start(ow_col[first:last, :], ow[0][first:last, :])
 
         out_map = keep.tile([P, T], F32, name="out_map", align_bytes=256)
         nc.vector.memset(out_map[:], 0.0)

@@ -59,8 +59,11 @@ def tile_attend_pre_diffscat_f_topk_kernel(tc, qT, kT, rT, ow, offs, out):
         k_got = [keep.tile([P, 2, N], F32, name=f"k_got{w}", align_bytes=256) for w in range(2)]
         r_got = [keep.tile([P, 2, N], F32, name="r_got0", align_bytes=256), shared.tile([P, 2, N], F32, name="r_got1", align_bytes=256, offset=2048)]
         u_low = keep.tile([P, 3, N], BF16, name="u_low", align_bytes=256)
-        u_words = [keep.tile([P, CHUNK, PACK], BF16, name=f"u_words{c}", align_bytes=256) for c in range(CHUNKS)]
-        u_codes = {c: keep.tile([P, CHUNK], U32, name=f"u_codes{c}", align_bytes=256) for c in (1, 3)}
+        words_31 = keep.tile([P, 2 * CHUNK, PACK], BF16, name="words_31", align_bytes=256)
+        u_words = {c: keep.tile([P, CHUNK, PACK], BF16, name=f"u_words{c}", align_bytes=256)[:] for c in (0, 2)}
+        u_words[3] = words_31[:, 0:CHUNK, :]
+        u_words[1] = words_31[:, CHUNK : 2 * CHUNK, :]
+        u_codes = {c: keep.tile([P, CHUNK], U32, name=f"u_codes{c}", align_bytes=256) for c in (1, 2, 3)}
         u_scales = [keep.tile([P, CHUNK], U8, name=f"u_scales{c}", align_bytes=256) for c in range(CHUNKS)]
         q_words = keep.tile([P, NQ, PACK], BF16, name="q_words", align_bytes=256)
         q_codes = keep.tile([P, NQ], U32, name="q_codes", align_bytes=256)
@@ -89,19 +92,24 @@ def tile_attend_pre_diffscat_f_topk_kernel(tc, qT, kT, rT, ow, offs, out):
                 out=codes[:].bitcast(FP8X4), scales=scales[:], in_=words[:].rearrange("p i t -> p (i t)")
             )
 
-        def project(c):
-            quantize(u_codes[c], u_scales[c], u_words[c])
-            acc = psum.tile([NQ, CHUNK], F32, name=f"acc{c}")
+        def project(c, first=0, last=CHUNK):
+            part = slice(first, last)
+            nc.vector.quantize_mx(
+                out=u_codes[c][:, part].bitcast(FP8X4),
+                scales=u_scales[c][:, part],
+                in_=u_words[c][:, part, :].rearrange("p i t -> p (i t)"),
+            )
+            acc = psum.tile([NQ, last - first], F32, name=f"acc{c}_{first}")
             nc.tensor.matmul_mx(
                 out=acc[:],
                 lhsT=q_codes[:].bitcast(FP8X4),
                 lhsT_scale=q_scales[:],
-                rhs=u_codes[c][:].bitcast(FP8X4),
-                rhs_scale=u_scales[c][:],
+                rhs=u_codes[c][:, part].bitcast(FP8X4),
+                rhs_scale=u_scales[c][:, part],
                 start=True,
                 stop=True,
             )
-            nc.scalar.activation(y[:, cols[c]], acc[:], COPY, scale=ow_col[:])
+            nc.scalar.activation(y[:, c * CHUNK + first : c * CHUNK + last], acc[:], COPY, scale=ow_col[:])
 
         for t in (0, 1):
             gather(k_got, k_win, t)
@@ -126,18 +134,19 @@ def tile_attend_pre_diffscat_f_topk_kernel(tc, qT, kT, rT, ow, offs, out):
             q_words[:].rearrange("p (c i) t -> p c t i", i=4), q_raw[:].rearrange("p t (c i) -> p c t i", i=4)
         )
         u_codes[0] = shared.tile([P, CHUNK], U32, name="u_codes0", align_bytes=256, offset=1024)
-        subtract_last(1)
+        last1 = keep.tile([P, CHUNK + 2], BF16, name="u_last1", align_bytes=256)
+        nc.vector.tensor_tensor(last1[:], k_got[1][:, 1, CHUNK - 2 : HALF], r_got[1][:, 1, CHUNK - 2 : HALF], SUB)
+        nc.scalar.copy(words_31[:, CHUNK - 2 : 2 * CHUNK, 3], last1[:])
         subtract_plane_in_place(0, 3)
         subtract_last(2)
         quantize(q_codes, q_scales, q_words)
-        project(0)
-        last3 = shared.tile([P, CHUNK], BF16, name="u_last3", align_bytes=256, offset=0)
-        nc.vector.tensor_tensor(last3[:], k_got[1][:, 1, cols[3]], r_got[1][:, 1, cols[3]], SUB)
+        project(0, 0, 64)
+        project(0, 64, CHUNK)
+        subtract_plane_in_place(3, 3)
         project(1)
-        nc.vector.tensor_copy(u_words[3][:, :, 3], last3[:])
-        u_codes[2] = shared.tile([P, CHUNK], U32, name="u_codes2", align_bytes=256, offset=2048)
         project(2)
-        project(3)
+        project(3, 0, 64)
+        project(3, 64, CHUNK)
         nc.vector.tensor_tensor(out_map[:].indirect(listed(0, CHUNK)), y[:, 0:CHUNK], zeros[:], ADD)
         nc.vector.tensor_copy(out_map[:].indirect(listed(CHUNK, N)), y[:, CHUNK:N])
         nc.sync.dma_start(out[0], out_map[:])

@@ -59,10 +59,10 @@ def tile_attend_pre_diffscat_f_topk_kernel(tc, qT, kT, rT, ow, offs, out):
         k_got = [keep.tile([P, 2, N], F32, name=f"k_got{w}", align_bytes=256) for w in range(2)]
         r_got = [keep.tile([P, 2, N], F32, name="r_got0", align_bytes=256), shared.tile([P, 2, N], F32, name="r_got1", align_bytes=256, offset=2048)]
         u_low = keep.tile([P, 3, N], BF16, name="u_low", align_bytes=256)
-        words_31 = keep.tile([P, 2 * CHUNK, PACK], BF16, name="words_31", align_bytes=256)
-        u_words = {c: keep.tile([P, CHUNK, PACK], BF16, name=f"u_words{c}", align_bytes=256)[:] for c in (0, 2)}
-        u_words[3] = words_31[:, 0:CHUNK, :]
-        u_words[1] = words_31[:, CHUNK : 2 * CHUNK, :]
+        words_03 = keep.tile([P, 2 * CHUNK, PACK], BF16, name="words_03", align_bytes=256)
+        u_words = {c: keep.tile([P, CHUNK, PACK], BF16, name=f"u_words{c}", align_bytes=256)[:] for c in (1, 2)}
+        u_words[0] = words_03[:, 0:CHUNK, :]
+        u_words[3] = words_03[:, CHUNK : 2 * CHUNK, :]
         u_codes = {c: keep.tile([P, CHUNK], U32, name=f"u_codes{c}", align_bytes=256) for c in (1, 2, 3)}
         u_scales = [keep.tile([P, CHUNK], U8, name=f"u_scales{c}", align_bytes=256) for c in range(CHUNKS)]
         q_words = keep.tile([P, NQ, PACK], BF16, name="q_words", align_bytes=256)
@@ -76,10 +76,10 @@ def tile_attend_pre_diffscat_f_topk_kernel(tc, qT, kT, rT, ow, offs, out):
         def gather(got, win, t, first=0, last=N):
             nc.vector.tensor_copy(got[t // 2][:, t % 2, first:last], win[t].indirect(listed(first, last)))
 
-        def subtract_last(c):
-            last = keep.tile([P, CHUNK], BF16, name=f"u_last{c}", align_bytes=256)
-            nc.vector.tensor_tensor(last[:], k_got[1][:, 1, cols[c]], r_got[1][:, 1, cols[c]], SUB)
-            nc.scalar.copy(u_words[c][:, :, 3], last[:])
+        def subtract_last(c, first, last, dense):
+            slots = slice(c * CHUNK + first, c * CHUNK + last)
+            nc.vector.tensor_tensor(dense[:], k_got[1][:, 1, slots], r_got[1][:, 1, slots], SUB)
+            nc.scalar.copy(u_words[c][:, first:last, 3], dense[:])
 
         def interleave(c, planes):
             nc.scalar.copy(u_words[c][:, :, 0:planes], u_low[:, 0:planes, cols[c]].rearrange("p t i -> p i t"))
@@ -134,18 +134,21 @@ def tile_attend_pre_diffscat_f_topk_kernel(tc, qT, kT, rT, ow, offs, out):
             q_words[:].rearrange("p (c i) t -> p c t i", i=4), q_raw[:].rearrange("p t (c i) -> p c t i", i=4)
         )
         u_codes[0] = shared.tile([P, CHUNK], U32, name="u_codes0", align_bytes=256, offset=1024)
-        last1 = keep.tile([P, CHUNK + 2], BF16, name="u_last1", align_bytes=256)
-        nc.vector.tensor_tensor(last1[:], k_got[1][:, 1, CHUNK - 2 : HALF], r_got[1][:, 1, CHUNK - 2 : HALF], SUB)
-        nc.scalar.copy(words_31[:, CHUNK - 2 : 2 * CHUNK, 3], last1[:])
-        subtract_plane_in_place(0, 3)
-        subtract_last(2)
+        last0 = keep.tile([P, 66], BF16, name="u_last0", align_bytes=256)
+        nc.vector.tensor_tensor(last0[:], k_got[1][:, 1, 64 : CHUNK + 2], r_got[1][:, 1, 64 : CHUNK + 2], SUB)
+        nc.scalar.copy(words_03[:, 64 : CHUNK + 2, 3], last0[:])
+        subtract_last(1, 0, CHUNK, keep.tile([P, CHUNK], BF16, name="u_last1", align_bytes=256))
+        nc.vector.tensor_tensor(u_words[0][:, 0:64, 3], k_got[1][:, 1, 0:64], r_got[1][:, 1, 0:64], SUB)
+        subtract_last(2, 0, 64, keep.tile([P, 64], BF16, name="u_last2a", align_bytes=256))
         quantize(q_codes, q_scales, q_words)
         project(0, 0, 64)
         project(0, 64, CHUNK)
+        subtract_last(2, 64, CHUNK, shared.tile([P, 64], BF16, name="u_last2b", align_bytes=256, offset=0))
         subtract_plane_in_place(3, 3)
         project(1)
-        project(2)
+        project(2, 0, 64)
         project(3, 0, 64)
+        project(2, 64, CHUNK)
         project(3, 64, CHUNK)
         nc.vector.tensor_tensor(out_map[:].indirect(listed(0, CHUNK)), y[:, 0:CHUNK], zeros[:], ADD)
         nc.vector.tensor_copy(out_map[:].indirect(listed(CHUNK, N)), y[:, CHUNK:N])

@@ -142,14 +142,13 @@ def tile_attend_pre_diffscat_f_topk_kernel(tc, qT, kT, rT, ow, offs, out):
         subtract_last(2, 0, 64, keep.tile([P, 64], BF16, name="u_last2a", align_bytes=256))
         quantize(q_codes, q_scales, q_words)
         project(0, 0, 64)
-        project(0, 64, CHUNK)
         subtract_last(2, 64, CHUNK, shared.tile([P, 64], BF16, name="u_last2b", align_bytes=256, offset=0))
+        project(0, 64, CHUNK)
         subtract_plane_in_place(3, 3)
         project(1)
         project(2, 0, 64)
-        project(3, 0, 64)
+        project(3)
         project(2, 64, CHUNK)
-        project(3, 64, CHUNK)
         nc.vector.tensor_tensor(out_map[:].indirect(listed(0, CHUNK)), y[:, 0:CHUNK], zeros[:], ADD)
         nc.vector.tensor_copy(out_map[:].indirect(listed(CHUNK, N)), y[:, CHUNK:N])
         nc.sync.dma_start(out[0], out_map[:])

@@ -21,23 +21,26 @@ LIST_ROWS = 16
 CHUNK = 128
 CHUNKS = N // CHUNK
 HALF = N // 2
+PIECES = (320, 384, 448, 448, 448)
 
 
 def tile_attend_pre_diffscat_f_topk_kernel(tc, qT, kT, rT, ow, offs, out):
     nc = tc.nc
     with ExitStack() as ctx:
         keep = ctx.enter_context(tc.tile_pool(name="keep", bufs=1))
-        shared = ctx.enter_context(tc.tile_pool(name="shared", bufs=1))
         psum = ctx.enter_context(tc.psum_pool(name="psum", bufs=1))
+
+        def tile(shape, dtype, name):
+            return keep.tile(shape, dtype, name=name, align_bytes=256)
 
         offsets = keep.tile([P, N // LIST_ROWS], U16, name="offsets")
         k_planes = kT.rearrange("(p t) c -> p t c", t=PACK)
         r_planes = rT.rearrange("(p t) c -> p t c", t=PACK)
-        k_head = keep.tile([P, 2, T], F32, name="k_head", align_bytes=256)
-        r_head = keep.tile([P, 2, T], F32, name="r_head", align_bytes=256)
-        k_win = [k_head[:, 0, :], k_head[:, 1, :]] + [keep.tile([P, T], F32, name=f"k_win{t}", align_bytes=256)[:] for t in (2, 3)]
-        r_win = [r_head[:, 0, :], r_head[:, 1, :]] + [keep.tile([P, T], F32, name=f"r_win{t}", align_bytes=256)[:] for t in (2, 3)]
-        q_raw = shared.tile([P, PACK, NQ], F32, name="q_raw", align_bytes=256, offset=0)
+        k_head = tile([P, 2, T], F32, "k_head")
+        r_head = tile([P, 2, T], F32, "r_head")
+        k_win = [k_head[:, 0, :], k_head[:, 1, :]] + [tile([P, T], F32, f"k_win{t}")[:] for t in (2, 3)]
+        r_win = [r_head[:, 0, :], r_head[:, 1, :]] + [tile([P, T], F32, f"r_win{t}")[:] for t in (2, 3)]
+        q_raw = tile([P, PACK, NQ], F32, "q_raw")
         ow_col = keep.tile([P, 1], F32, name="ow_col")
 
         nc.sync.dma_start(k_head[:], k_planes[:, 0:2, :])
@@ -47,108 +50,94 @@ def tile_attend_pre_diffscat_f_topk_kernel(tc, qT, kT, rT, ow, offs, out):
             nc.sync.dma_start(k_win[t], k_planes[:, t, :])
             nc.sync.dma_start(r_win[t], r_planes[:, t, :])
         nc.sync.dma_start(q_raw[:], qT[0].rearrange("(p t) q -> p t q", t=PACK))
-        for first, last in ((0, 32), (32, 64), (64, 80), (80, 96), (96, 112), (112, 128)):
-            nc.sync.dma_start(ow_col[first:last, :], ow[0][first:last, :])
+        nc.sync.dma_start(ow_col[:], ow[0])
 
-        out_map = keep.tile([P, T], F32, name="out_map", align_bytes=256)
-        nc.vector.memset(out_map[:], 0.0)
-        zeros = keep.tile([P, CHUNK], F32, name="zeros", align_bytes=256)
+        maps = [tile([P, T], F32, f"map{h}") for h in range(2)]
+        for h in range(2):
+            nc.vector.memset(maps[h][:], 0.0)
+        zeros = tile([P, CHUNK], F32, "zeros")
         nc.vector.memset(zeros[:], 0.0)
 
         cols = [slice(c * CHUNK, (c + 1) * CHUNK) for c in range(CHUNKS)]
-        k_got = [keep.tile([P, 2, N], F32, name=f"k_got{w}", align_bytes=256) for w in range(2)]
-        r_got = [keep.tile([P, 2, N], F32, name="r_got0", align_bytes=256), shared.tile([P, 2, N], F32, name="r_got1", align_bytes=256, offset=2048)]
-        u_low = keep.tile([P, 3, N], BF16, name="u_low", align_bytes=256)
-        words_03 = keep.tile([P, 2 * CHUNK, PACK], BF16, name="words_03", align_bytes=256)
-        u_words = {c: keep.tile([P, CHUNK, PACK], BF16, name=f"u_words{c}", align_bytes=256)[:] for c in (1, 2)}
-        u_words[0] = words_03[:, 0:CHUNK, :]
-        u_words[3] = words_03[:, CHUNK : 2 * CHUNK, :]
-        u_codes = {c: keep.tile([P, CHUNK], U32, name=f"u_codes{c}", align_bytes=256) for c in (1, 2, 3)}
-        u_scales = [keep.tile([P, CHUNK], U8, name=f"u_scales{c}", align_bytes=256) for c in range(CHUNKS)]
-        q_words = keep.tile([P, NQ, PACK], BF16, name="q_words", align_bytes=256)
-        q_codes = keep.tile([P, NQ], U32, name="q_codes", align_bytes=256)
-        q_scales = keep.tile([P, NQ], U8, name="q_scales", align_bytes=256)
-        y = keep.tile([NQ, N], F32, name="y", align_bytes=256)
+        k_low = tile([P, 2, N], F32, "k_low")
+        r_low = tile([P, 2, N], F32, "r_low")
+        k_got = {t: tile([P, N], F32, f"k_got{t}") for t in (2, 3)}
+        r_got2 = tile([P, N], F32, "r_got2")
+        r_last = [tile([P, CHUNK], F32, "r_last0"), tile([P, CHUNK], F32, "r_last1"), tile([P, HALF], F32, "r_last23")]
+        u_low = tile([P, 3, N], BF16, "u_low")
+        u_last = tile([P, HALF], BF16, "u_last")
+        u_words = [tile([P, CHUNK, PACK], BF16, f"u_words{c}") for c in range(CHUNKS)]
+        u_codes = [tile([P, CHUNK], U32, f"u_codes{c}") for c in range(CHUNKS)]
+        u_scales = [tile([P, CHUNK], U8, f"u_scales{c}") for c in range(CHUNKS)]
+        q_words = tile([P, NQ, PACK], BF16, "q_words")
+        q_codes = tile([P, NQ], U32, "q_codes")
+        q_scales = tile([P, NQ], U8, "q_scales")
+        acc = [psum.tile([NQ, CHUNK], F32, name=f"acc{c}") for c in range(CHUNKS)]
+        y = tile([NQ, N], F32, "y")
 
         def listed(first, last):
             return offsets[:, first // LIST_ROWS : last // LIST_ROWS]
-
-        def gather(got, win, t, first=0, last=N):
-            nc.vector.tensor_copy(got[t // 2][:, t % 2, first:last], win[t].indirect(listed(first, last)))
-
-        def subtract_last(c, first, last, dense):
-            slots = slice(c * CHUNK + first, c * CHUNK + last)
-            nc.vector.tensor_tensor(dense[:], k_got[1][:, 1, slots], r_got[1][:, 1, slots], SUB)
-            nc.scalar.copy(u_words[c][:, first:last, 3], dense[:])
-
-        def interleave(c, planes):
-            nc.scalar.copy(u_words[c][:, :, 0:planes], u_low[:, 0:planes, cols[c]].rearrange("p t i -> p i t"))
-
-        def subtract_plane_in_place(c, t):
-            nc.vector.tensor_tensor(u_words[c][:, :, t], k_got[1][:, t % 2, cols[c]], r_got[1][:, t % 2, cols[c]], SUB)
 
         def quantize(codes, scales, words):
             nc.vector.quantize_mx(
                 out=codes[:].bitcast(FP8X4), scales=scales[:], in_=words[:].rearrange("p i t -> p (i t)")
             )
 
-        def project(c, first=0, last=CHUNK):
-            part = slice(first, last)
-            nc.vector.quantize_mx(
-                out=u_codes[c][:, part].bitcast(FP8X4),
-                scales=u_scales[c][:, part],
-                in_=u_words[c][:, part, :].rearrange("p i t -> p (i t)"),
-            )
-            acc = psum.tile([NQ, last - first], F32, name=f"acc{c}_{first}")
+        def multiply(c):
             nc.tensor.matmul_mx(
-                out=acc[:],
+                out=acc[c][:],
                 lhsT=q_codes[:].bitcast(FP8X4),
                 lhsT_scale=q_scales[:],
-                rhs=u_codes[c][:, part].bitcast(FP8X4),
-                rhs_scale=u_scales[c][:, part],
+                rhs=u_codes[c][:].bitcast(FP8X4),
+                rhs_scale=u_scales[c][:],
                 start=True,
                 stop=True,
             )
-            nc.scalar.activation(y[:, c * CHUNK + first : c * CHUNK + last], acc[:], COPY, scale=ow_col[:])
+
+        def place(c, planes):
+            nc.scalar.copy(u_words[c][:, :, 0:planes], u_low[:, 0:planes, cols[c]].rearrange("p t i -> p i t"))
 
         for t in (0, 1):
-            gather(k_got, k_win, t)
+            nc.vector.tensor_copy(k_low[:, t, :], k_win[t].indirect(offsets[:]))
         for t in (0, 1):
-            gather(r_got, r_win, t)
-        nc.vector.tensor_tensor(u_low[:, 0:2, :], k_got[0][:], r_got[0][:], SUB)
-        interleave(0, 2)
-        interleave(3, 2)
-        gather(k_got, k_win, 2)
-        gather(r_got, r_win, 2)
-        middle = slice(CHUNK, 3 * CHUNK)
-        nc.vector.tensor_tensor(u_low[:, 2, middle], k_got[1][:, 0, middle], r_got[1][:, 0, middle], SUB)
-        for c in (1, 2):
-            interleave(c, 3)
-        subtract_plane_in_place(0, 2)
-        subtract_plane_in_place(3, 2)
-        gather(k_got, k_win, 3)
+            nc.vector.tensor_copy(r_low[:, t, :], r_win[t].indirect(offsets[:]))
+        nc.vector.tensor_tensor(u_low[:, 0:2, :], k_low[:], r_low[:], SUB)
+        nc.scalar.activation(k_got[2][:], k_win[2].indirect(offsets[:]), COPY)
+        for c in (0, 1):
+            place(c, 2)
+        nc.vector.tensor_copy(r_got2[:], r_win[2].indirect(offsets[:]))
+        nc.vector.tensor_tensor(u_low[:, 2, HALF:N], k_got[2][:, HALF:N], r_got2[:, HALF:N], SUB)
+        for c in (0, 1):
+            nc.vector.tensor_tensor(u_words[c][:, :, 2], k_got[2][:, cols[c]], r_got2[:, cols[c]], SUB)
+        for c in (2, 3):
+            place(c, 3)
+        nc.vector.tensor_copy(k_got[3][:], k_win[3].indirect(offsets[:]))
 
-        gather(r_got, r_win, 3, 0, HALF)
-        gather(r_got, r_win, 3, HALF, N)
+        for c in (0, 1):
+            nc.vector.tensor_copy(r_last[c][:], r_win[3].indirect(listed(c * CHUNK, (c + 1) * CHUNK)))
+        nc.scalar.activation(r_last[2][:], r_win[3].indirect(listed(HALF, N)), COPY)
         nc.scalar.copy(
             q_words[:].rearrange("p (c i) t -> p c t i", i=4), q_raw[:].rearrange("p t (c i) -> p c t i", i=4)
         )
-        u_codes[0] = shared.tile([P, CHUNK], U32, name="u_codes0", align_bytes=256, offset=1024)
-        last0 = keep.tile([P, 66], BF16, name="u_last0", align_bytes=256)
-        nc.vector.tensor_tensor(last0[:], k_got[1][:, 1, 64 : CHUNK + 2], r_got[1][:, 1, 64 : CHUNK + 2], SUB)
-        nc.scalar.copy(words_03[:, 64 : CHUNK + 2, 3], last0[:])
-        subtract_last(1, 0, CHUNK, keep.tile([P, CHUNK], BF16, name="u_last1", align_bytes=256))
-        nc.vector.tensor_tensor(u_words[0][:, 0:64, 3], k_got[1][:, 1, 0:64], r_got[1][:, 1, 0:64], SUB)
-        subtract_last(2, 0, 64, keep.tile([P, 64], BF16, name="u_last2a", align_bytes=256))
+        nc.vector.tensor_tensor(u_words[0][:, :, 3], k_got[3][:, cols[0]], r_last[0][:], SUB)
+        nc.vector.tensor_tensor(u_last[:], k_got[3][:, HALF:N], r_last[2][:], SUB)
+        for c in (2, 3):
+            nc.scalar.copy(u_words[c][:, :, 3], u_last[:, cols[c - 2]])
+        quantize(u_codes[0], u_scales[0], u_words[0])
         quantize(q_codes, q_scales, q_words)
-        project(0, 0, 64)
-        subtract_last(2, 64, CHUNK, shared.tile([P, 64], BF16, name="u_last2b", align_bytes=256, offset=0))
-        project(0, 64, CHUNK)
-        subtract_plane_in_place(3, 3)
-        project(1)
-        project(2, 0, 64)
-        project(3)
-        project(2, 64, CHUNK)
-        nc.vector.tensor_tensor(out_map[:].indirect(listed(0, CHUNK)), y[:, 0:CHUNK], zeros[:], ADD)
-        nc.vector.tensor_copy(out_map[:].indirect(listed(CHUNK, N)), y[:, CHUNK:N])
-        nc.sync.dma_start(out[0], out_map[:])
+        nc.vector.tensor_tensor(u_words[1][:, :, 3], k_got[3][:, cols[1]], r_last[1][:], SUB)
+        for c in (2, 1, 3):
+            quantize(u_codes[c], u_scales[c], u_words[c])
+        for c in (0, 2, 1, 3):
+            multiply(c)
+            nc.scalar.activation(y[:, cols[c]], acc[c][:], COPY, scale=ow_col[:])
+        nc.vector.tensor_tensor(maps[1][:].indirect(listed(0, CHUNK)), y[:, cols[0]], zeros[:], ADD)
+        nc.scalar.activation(maps[0][:].indirect(listed(CHUNK, 3 * CHUNK)), y[:, CHUNK : 3 * CHUNK], COPY)
+        nc.vector.tensor_tensor(maps[1][:].indirect(listed(3 * CHUNK, N)), y[:, cols[3]], zeros[:], ADD)
+
+        for n, width in enumerate(PIECES):
+            first = sum(PIECES[:n])
+            piece = slice(first, first + width)
+            both = tile([P, width], F32, f"both{first}")
+            nc.vector.tensor_tensor(both[:], maps[0][:, piece], maps[1][:, piece], ADD)
+            nc.sync.dma_start(out[0][:, piece], both[:])

@@ -28,6 +28,7 @@ def tile_attend_pre_diffscat_f_topk_kernel(tc, qT, kT, rT, ow, offs, out):
     nc = tc.nc
     with ExitStack() as ctx:
         keep = ctx.enter_context(tc.tile_pool(name="keep", bufs=1))
+        shared = ctx.enter_context(tc.tile_pool(name="shared", bufs=1))
         psum = ctx.enter_context(tc.psum_pool(name="psum", bufs=1))
 
         def tile(shape, dtype, name):
@@ -36,19 +37,19 @@ def tile_attend_pre_diffscat_f_topk_kernel(tc, qT, kT, rT, ow, offs, out):
         offsets = keep.tile([P, N // LIST_ROWS], U16, name="offsets")
         k_planes = kT.rearrange("(p t) c -> p t c", t=PACK)
         r_planes = rT.rearrange("(p t) c -> p t c", t=PACK)
-        k_head = tile([P, 2, T], F32, "k_head")
+        k_head = tile([P, 3, T], F32, "k_head")
         r_head = tile([P, 2, T], F32, "r_head")
-        k_win = [k_head[:, 0, :], k_head[:, 1, :]] + [tile([P, T], F32, f"k_win{t}")[:] for t in (2, 3)]
+        k_win = [k_head[:, t, :] for t in range(3)] + [tile([P, T], F32, "k_win3")[:]]
         r_win = [r_head[:, 0, :], r_head[:, 1, :]] + [tile([P, T], F32, f"r_win{t}")[:] for t in (2, 3)]
-        q_raw = tile([P, PACK, NQ], F32, "q_raw")
+        q_raw = shared.tile([P, PACK, NQ], F32, name="q_raw", align_bytes=256, offset=0)
         ow_col = keep.tile([P, 1], F32, name="ow_col")
 
-        nc.sync.dma_start(k_head[:], k_planes[:, 0:2, :])
+        nc.sync.dma_start(k_head[:], k_planes[:, 0:3, :])
         nc.sync.dma_start(offsets[:], offs)
         nc.sync.dma_start(r_head[:], r_planes[:, 0:2, :])
-        for t in (2, 3):
-            nc.sync.dma_start(k_win[t], k_planes[:, t, :])
-            nc.sync.dma_start(r_win[t], r_planes[:, t, :])
+        nc.sync.dma_start(r_win[2], r_planes[:, 2, :])
+        nc.sync.dma_start(k_win[3], k_planes[:, 3, :])
+        nc.sync.dma_start(r_win[3], r_planes[:, 3, :])
         nc.sync.dma_start(q_raw[:], qT[0].rearrange("(p t) q -> p t q", t=PACK))
         nc.sync.dma_start(ow_col[:], ow[0])
 
@@ -63,11 +64,14 @@ def tile_attend_pre_diffscat_f_topk_kernel(tc, qT, kT, rT, ow, offs, out):
         r_low = tile([P, 2, N], F32, "r_low")
         k_got = {t: tile([P, N], F32, f"k_got{t}") for t in (2, 3)}
         r_got2 = tile([P, N], F32, "r_got2")
-        r_last = [tile([P, CHUNK], F32, "r_last0"), tile([P, CHUNK], F32, "r_last1"), tile([P, HALF], F32, "r_last23")]
+        r_first = tile([P, HALF], F32, "r_first")
+        r_last = [r_first[:, cols[0]], r_first[:, cols[1]]] + [tile([P, CHUNK], F32, f"r_last{c}")[:] for c in (2, 3)]
         u_low = tile([P, 3, N], BF16, "u_low")
-        u_last = tile([P, HALF], BF16, "u_last")
+        u_last = {c: tile([P, CHUNK], BF16, f"u_last{c}") for c in (2, 3)}
         u_words = [tile([P, CHUNK, PACK], BF16, f"u_words{c}") for c in range(CHUNKS)]
-        u_codes = [tile([P, CHUNK], U32, f"u_codes{c}") for c in range(CHUNKS)]
+        u_codes = [
+            shared.tile([P, CHUNK], U32, name=f"u_codes{c}", align_bytes=256, offset=4 * c * CHUNK) for c in range(CHUNKS)
+        ]
         u_scales = [tile([P, CHUNK], U8, f"u_scales{c}") for c in range(CHUNKS)]
         q_words = tile([P, NQ, PACK], BF16, "q_words")
         q_codes = tile([P, NQ], U32, "q_codes")
@@ -97,12 +101,12 @@ def tile_attend_pre_diffscat_f_topk_kernel(tc, qT, kT, rT, ow, offs, out):
         def place(c, planes):
             nc.scalar.copy(u_words[c][:, :, 0:planes], u_low[:, 0:planes, cols[c]].rearrange("p t i -> p i t"))
 
-        for t in (0, 1):
-            nc.vector.tensor_copy(k_low[:, t, :], k_win[t].indirect(offsets[:]))
-        for t in (0, 1):
-            nc.vector.tensor_copy(r_low[:, t, :], r_win[t].indirect(offsets[:]))
+        nc.vector.tensor_copy(k_low[:, 0, :], k_win[0].indirect(offsets[:]))
+        nc.scalar.activation(k_low[:, 1, :], k_win[1].indirect(offsets[:]), COPY)
+        nc.vector.tensor_copy(k_got[2][:], k_win[2].indirect(offsets[:]))
+        nc.vector.tensor_copy(r_low[:, 0, :], r_win[0].indirect(offsets[:]))
+        nc.scalar.activation(r_low[:, 1, :], r_win[1].indirect(offsets[:]), COPY)
         nc.vector.tensor_tensor(u_low[:, 0:2, :], k_low[:], r_low[:], SUB)
-        nc.scalar.activation(k_got[2][:], k_win[2].indirect(offsets[:]), COPY)
         for c in (0, 1):
             place(c, 2)
         nc.vector.tensor_copy(r_got2[:], r_win[2].indirect(offsets[:]))
@@ -113,19 +117,18 @@ def tile_attend_pre_diffscat_f_topk_kernel(tc, qT, kT, rT, ow, offs, out):
             place(c, 3)
         nc.vector.tensor_copy(k_got[3][:], k_win[3].indirect(offsets[:]))
 
-        for c in (0, 1):
-            nc.vector.tensor_copy(r_last[c][:], r_win[3].indirect(listed(c * CHUNK, (c + 1) * CHUNK)))
-        nc.scalar.activation(r_last[2][:], r_win[3].indirect(listed(HALF, N)), COPY)
+        for c in (2, 3):
+            nc.vector.tensor_copy(r_last[c], r_win[3].indirect(listed(c * CHUNK, (c + 1) * CHUNK)))
+        nc.scalar.activation(r_first[:], r_win[3].indirect(listed(0, HALF)), COPY)
         nc.scalar.copy(
             q_words[:].rearrange("p (c i) t -> p c t i", i=4), q_raw[:].rearrange("p t (c i) -> p c t i", i=4)
         )
-        nc.vector.tensor_tensor(u_words[0][:, :, 3], k_got[3][:, cols[0]], r_last[0][:], SUB)
-        nc.vector.tensor_tensor(u_last[:], k_got[3][:, HALF:N], r_last[2][:], SUB)
-        for c in (2, 3):
-            nc.scalar.copy(u_words[c][:, :, 3], u_last[:, cols[c - 2]])
+        for c in (0, 1):
+            nc.vector.tensor_tensor(u_last[c + 2][:], k_got[3][:, cols[c + 2]], r_last[c + 2], SUB)
+            nc.scalar.copy(u_words[c + 2][:, :, 3], u_last[c + 2][:])
+            nc.vector.tensor_tensor(u_words[c][:, :, 3], k_got[3][:, cols[c]], r_last[c], SUB)
         quantize(u_codes[0], u_scales[0], u_words[0])
         quantize(q_codes, q_scales, q_words)
-        nc.vector.tensor_tensor(u_words[1][:, :, 3], k_got[3][:, cols[1]], r_last[1][:], SUB)
         for c in (2, 1, 3):
             quantize(u_codes[c], u_scales[c], u_words[c])
         for c in (0, 2, 1, 3):

@@ -37,19 +37,19 @@ def tile_attend_pre_diffscat_f_topk_kernel(tc, qT, kT, rT, ow, offs, out):
         offsets = keep.tile([P, N // LIST_ROWS], U16, name="offsets")
         k_planes = kT.rearrange("(p t) c -> p t c", t=PACK)
         r_planes = rT.rearrange("(p t) c -> p t c", t=PACK)
-        k_head = tile([P, 3, T], F32, "k_head")
+        k_head = tile([P, 2, T], F32, "k_head")
         r_head = tile([P, 2, T], F32, "r_head")
-        k_win = [k_head[:, t, :] for t in range(3)] + [tile([P, T], F32, "k_win3")[:]]
+        k_win = [k_head[:, 0, :], k_head[:, 1, :]] + [tile([P, T], F32, f"k_win{t}")[:] for t in (2, 3)]
         r_win = [r_head[:, 0, :], r_head[:, 1, :]] + [tile([P, T], F32, f"r_win{t}")[:] for t in (2, 3)]
         q_raw = shared.tile([P, PACK, NQ], F32, name="q_raw", align_bytes=256, offset=0)
         ow_col = keep.tile([P, 1], F32, name="ow_col")
 
-        nc.sync.dma_start(k_head[:], k_planes[:, 0:3, :])
+        nc.sync.dma_start(k_head[:], k_planes[:, 0:2, :])
         nc.sync.dma_start(offsets[:], offs)
         nc.sync.dma_start(r_head[:], r_planes[:, 0:2, :])
-        nc.sync.dma_start(r_win[2], r_planes[:, 2, :])
-        nc.sync.dma_start(k_win[3], k_planes[:, 3, :])
-        nc.sync.dma_start(r_win[3], r_planes[:, 3, :])
+        for t in (2, 3):
+            nc.sync.dma_start(k_win[t], k_planes[:, t, :])
+            nc.sync.dma_start(r_win[t], r_planes[:, t, :])
         nc.sync.dma_start(q_raw[:], qT[0].rearrange("(p t) q -> p t q", t=PACK))
         nc.sync.dma_start(ow_col[:], ow[0])
 
@@ -103,10 +103,10 @@ def tile_attend_pre_diffscat_f_topk_kernel(tc, qT, kT, rT, ow, offs, out):
 
         nc.vector.tensor_copy(k_low[:, 0, :], k_win[0].indirect(offsets[:]))
         nc.scalar.activation(k_low[:, 1, :], k_win[1].indirect(offsets[:]), COPY)
-        nc.vector.tensor_copy(k_got[2][:], k_win[2].indirect(offsets[:]))
         nc.vector.tensor_copy(r_low[:, 0, :], r_win[0].indirect(offsets[:]))
         nc.scalar.activation(r_low[:, 1, :], r_win[1].indirect(offsets[:]), COPY)
         nc.vector.tensor_tensor(u_low[:, 0:2, :], k_low[:], r_low[:], SUB)
+        nc.vector.tensor_copy(k_got[2][:], k_win[2].indirect(offsets[:]))
         for c in (0, 1):
             place(c, 2)
         nc.vector.tensor_copy(r_got2[:], r_win[2].indirect(offsets[:]))

@@ -46,12 +46,12 @@ def tile_attend_pre_diffscat_f_topk_kernel(tc, qT, kT, rT, ow, offs, out):
 
         nc.sync.dma_start(k_head[:], k_planes[:, 0:2, :])
         nc.sync.dma_start(offsets[:], offs)
+        nc.sync.dma_start(ow_col[:], ow[0])
         nc.sync.dma_start(r_head[:], r_planes[:, 0:2, :])
         for t in (2, 3):
             nc.sync.dma_start(k_win[t], k_planes[:, t, :])
             nc.sync.dma_start(r_win[t], r_planes[:, t, :])
         nc.sync.dma_start(q_raw[:], qT[0].rearrange("(p t) q -> p t q", t=PACK))
-        nc.sync.dma_start(ow_col[:], ow[0])
 
         maps = [tile([P, T], F32, f"map{h}") for h in range(2)]
         for h in range(2):
@@ -64,14 +64,15 @@ def tile_attend_pre_diffscat_f_topk_kernel(tc, qT, kT, rT, ow, offs, out):
         r_low = tile([P, 2, N], F32, "r_low")
         k_got = {t: tile([P, N], F32, f"k_got{t}") for t in (2, 3)}
         r_got2 = tile([P, N], F32, "r_got2")
-        r_first = tile([P, HALF], F32, "r_first")
-        r_last = [r_first[:, cols[0]], r_first[:, cols[1]]] + [tile([P, CHUNK], F32, f"r_last{c}")[:] for c in (2, 3)]
+        r_last = [tile([P, CHUNK], F32, f"r_last{c}") for c in range(3)]
+        r_last.append(shared.tile([P, CHUNK], F32, name="r_last3", align_bytes=256, offset=3 * 4 * CHUNK))
         u_low = tile([P, 3, N], BF16, "u_low")
-        u_last = {c: tile([P, CHUNK], BF16, f"u_last{c}") for c in (2, 3)}
+        u_last = tile([P, CHUNK], BF16, "u_last")
         u_words = [tile([P, CHUNK, PACK], BF16, f"u_words{c}") for c in range(CHUNKS)]
         u_codes = [
-            shared.tile([P, CHUNK], U32, name=f"u_codes{c}", align_bytes=256, offset=4 * c * CHUNK) for c in range(CHUNKS)
+            shared.tile([P, CHUNK], U32, name=f"u_codes{c}", align_bytes=256, offset=4 * c * CHUNK) for c in range(3)
         ]
+        u_codes.append(tile([P, CHUNK], U32, "u_codes3"))
         u_scales = [tile([P, CHUNK], U8, f"u_scales{c}") for c in range(CHUNKS)]
         q_words = tile([P, NQ, PACK], BF16, "q_words")
         q_codes = tile([P, NQ], U32, "q_codes")
@@ -107,35 +108,45 @@ def tile_attend_pre_diffscat_f_topk_kernel(tc, qT, kT, rT, ow, offs, out):
         nc.scalar.activation(r_low[:, 1, :], r_win[1].indirect(offsets[:]), COPY)
         nc.vector.tensor_tensor(u_low[:, 0:2, :], k_low[:], r_low[:], SUB)
         nc.vector.tensor_copy(k_got[2][:], k_win[2].indirect(offsets[:]))
-        for c in (0, 1):
+        for c in (0, 1, 3):
             place(c, 2)
         nc.vector.tensor_copy(r_got2[:], r_win[2].indirect(offsets[:]))
-        nc.vector.tensor_tensor(u_low[:, 2, HALF:N], k_got[2][:, HALF:N], r_got2[:, HALF:N], SUB)
-        for c in (0, 1):
+        nc.vector.tensor_tensor(u_low[:, 2, cols[2]], k_got[2][:, cols[2]], r_got2[:, cols[2]], SUB)
+        for c in (0, 1, 3):
             nc.vector.tensor_tensor(u_words[c][:, :, 2], k_got[2][:, cols[c]], r_got2[:, cols[c]], SUB)
-        for c in (2, 3):
-            place(c, 3)
-        nc.vector.tensor_copy(k_got[3][:], k_win[3].indirect(offsets[:]))
+        place(2, 3)
+        nc.scalar.activation(k_got[3][:], k_win[3].indirect(offsets[:]), COPY)
 
-        for c in (2, 3):
-            nc.vector.tensor_copy(r_last[c], r_win[3].indirect(listed(c * CHUNK, (c + 1) * CHUNK)))
-        nc.scalar.activation(r_first[:], r_win[3].indirect(listed(0, HALF)), COPY)
+        def gather_last(c):
+            return r_win[3].indirect(listed(c * CHUNK, (c + 1) * CHUNK))
+
+        def subtract_last(c):
+            nc.vector.tensor_tensor(u_words[c][:, :, 3], k_got[3][:, cols[c]], r_last[c][:], SUB)
+
+        nc.vector.tensor_copy(r_last[2][:], gather_last(2))
+        for c in (0, 1):
+            nc.scalar.activation(r_last[c][:], gather_last(c), COPY)
         nc.scalar.copy(
             q_words[:].rearrange("p (c i) t -> p c t i", i=4), q_raw[:].rearrange("p t (c i) -> p c t i", i=4)
         )
+        nc.vector.tensor_tensor(u_last[:], k_got[3][:, cols[2]], r_last[2][:], SUB)
+        nc.scalar.copy(u_words[2][:, :, 3], u_last[:])
+        nc.scalar.activation(r_last[3][:], gather_last(3), COPY)
         for c in (0, 1):
-            nc.vector.tensor_tensor(u_last[c + 2][:], k_got[3][:, cols[c + 2]], r_last[c + 2], SUB)
-            nc.scalar.copy(u_words[c + 2][:, :, 3], u_last[c + 2][:])
-            nc.vector.tensor_tensor(u_words[c][:, :, 3], k_got[3][:, cols[c]], r_last[c], SUB)
+            subtract_last(c)
         quantize(u_codes[0], u_scales[0], u_words[0])
         quantize(q_codes, q_scales, q_words)
-        for c in (2, 1, 3):
+        for c in (1, 2):
             quantize(u_codes[c], u_scales[c], u_words[c])
-        for c in (0, 2, 1, 3):
+        subtract_last(3)
+        quantize(u_codes[3], u_scales[3], u_words[3])
+        for c in range(CHUNKS):
             multiply(c)
+        for c in range(3):
             nc.scalar.activation(y[:, cols[c]], acc[c][:], COPY, scale=ow_col[:])
         nc.vector.tensor_tensor(maps[1][:].indirect(listed(0, CHUNK)), y[:, cols[0]], zeros[:], ADD)
         nc.scalar.activation(maps[0][:].indirect(listed(CHUNK, 3 * CHUNK)), y[:, CHUNK : 3 * CHUNK], COPY)
+        nc.vector.tensor_scalar_mul(y[:, cols[3]], acc[3][:], ow_col[:])
         nc.vector.tensor_tensor(maps[1][:].indirect(listed(3 * CHUNK, N)), y[:, cols[3]], zeros[:], ADD)
 
         for n, width in enumerate(PIECES):

@@ -21,7 +21,8 @@ LIST_ROWS = 16
 CHUNK = 128
 CHUNKS = N // CHUNK
 HALF = N // 2
-PIECES = (320, 384, 448, 448, 448)
+BLOCK = 32
+PIECES = (192, 256, 320, 384, 448, 448)
 
 
 def tile_attend_pre_diffscat_f_topk_kernel(tc, qT, kT, rT, ow, offs, out):
@@ -42,17 +43,21 @@ def tile_attend_pre_diffscat_f_topk_kernel(tc, qT, kT, rT, ow, offs, out):
         k_win = [k_head[:, 0, :], k_head[:, 1, :]] + [tile([P, T], F32, f"k_win{t}")[:] for t in (2, 3)]
         r_win = [r_head[:, 0, :], r_head[:, 1, :]] + [tile([P, T], F32, f"r_win{t}")[:] for t in (2, 3)]
         q_raw = shared.tile([P, PACK, NQ], F32, name="q_raw", align_bytes=256, offset=0)
-        ow_col = keep.tile([P, 1], F32, name="ow_col")
+        ow_rows = tile([P, BLOCK], F32, "ow_rows")
+        ow_cols = tile([P, BLOCK], F32, "ow_cols")
+        ow_col = ow_cols[:, 0:1]
+        nc.vector.memset(ow_rows[:], 0.0)
 
         nc.sync.dma_start(k_head[:], k_planes[:, 0:2, :])
         nc.sync.dma_start(offsets[:], offs)
-        nc.sync.dma_start(ow_col[:], ow[0])
+        nc.sync.dma_start(ow_rows[0:P:BLOCK, :], ow[0].rearrange("(b i) o -> b (i o)", i=BLOCK))
         nc.sync.dma_start(r_head[:], r_planes[:, 0:2, :])
         for t in (2, 3):
             nc.sync.dma_start(k_win[t], k_planes[:, t, :])
             nc.sync.dma_start(r_win[t], r_planes[:, t, :])
         nc.sync.dma_start(q_raw[:], qT[0].rearrange("(p t) q -> p t q", t=PACK))
 
+        nc.vector.transpose(ow_cols[:], ow_rows[:])
         maps = [tile([P, T], F32, f"map{h}") for h in range(2)]
         for h in range(2):
             nc.vector.memset(maps[h][:], 0.0)
@@ -143,10 +148,10 @@ def tile_attend_pre_diffscat_f_topk_kernel(tc, qT, kT, rT, ow, offs, out):
         for c in range(CHUNKS):
             multiply(c)
         for c in range(3):
-            nc.scalar.activation(y[:, cols[c]], acc[c][:], COPY, scale=ow_col[:])
+            nc.scalar.activation(y[:, cols[c]], acc[c][:], COPY, scale=ow_col)
         nc.vector.tensor_tensor(maps[1][:].indirect(listed(0, CHUNK)), y[:, cols[0]], zeros[:], ADD)
         nc.scalar.activation(maps[0][:].indirect(listed(CHUNK, 3 * CHUNK)), y[:, CHUNK : 3 * CHUNK], COPY)
-        nc.vector.tensor_scalar_mul(y[:, cols[3]], acc[3][:], ow_col[:])
+        nc.vector.tensor_scalar_mul(y[:, cols[3]], acc[3][:], ow_col)
         nc.vector.tensor_tensor(maps[1][:].indirect(listed(3 * CHUNK, N)), y[:, cols[3]], zeros[:], ADD)
 
         for n, width in enumerate(PIECES):

@@ -128,9 +128,9 @@ def tile_attend_pre_diffscat_f_topk_kernel(tc, qT, kT, rT, ow, offs, out):
         def subtract_last(c):
             nc.vector.tensor_tensor(u_words[c][:, :, 3], k_got[3][:, cols[c]], r_last[c][:], SUB)
 
-        nc.vector.tensor_copy(r_last[2][:], gather_last(2))
-        for c in (0, 1):
-            nc.scalar.activation(r_last[c][:], gather_last(c), COPY)
+        for c in (2, 1):
+            nc.vector.tensor_copy(r_last[c][:], gather_last(c))
+        nc.scalar.activation(r_last[0][:], gather_last(0), COPY)
         nc.scalar.copy(
             q_words[:].rearrange("p (c i) t -> p c t i", i=4), q_raw[:].rearrange("p t (c i) -> p c t i", i=4)
         )

@@ -36,25 +36,23 @@ def tile_attend_pre_diffscat_f_topk_kernel(tc, qT, kT, rT, ow, offs, out):
             return keep.tile(shape, dtype, name=name, align_bytes=256)
 
         offsets = keep.tile([P, N // LIST_ROWS], U16, name="offsets")
-        k_planes = kT.rearrange("(p t) c -> p t c", t=PACK)
         r_planes = rT.rearrange("(p t) c -> p t c", t=PACK)
-        k_head = tile([P, 2, T], F32, "k_head")
+        k_win = tile([P, PACK, T], F32, "k_win")
         r_head = tile([P, 2, T], F32, "r_head")
-        k_win = [k_head[:, 0, :], k_head[:, 1, :]] + [tile([P, T], F32, f"k_win{t}")[:] for t in (2, 3)]
-        r_win = [r_head[:, 0, :], r_head[:, 1, :]] + [tile([P, T], F32, f"r_win{t}")[:] for t in (2, 3)]
+        r_win2 = tile([P, T], F32, "r_win2")
+        r_win3 = tile([P, T], F32, "r_win3")
         q_raw = shared.tile([P, PACK, NQ], F32, name="q_raw", align_bytes=256, offset=0)
         ow_rows = tile([P, BLOCK], F32, "ow_rows")
         ow_cols = tile([P, BLOCK], F32, "ow_cols")
         ow_col = ow_cols[:, 0:1]
         nc.vector.memset(ow_rows[:], 0.0)
 
-        nc.sync.dma_start(k_head[:], k_planes[:, 0:2, :])
+        nc.sync.dma_start(k_win[:], kT.rearrange("(p t) c -> p t c", t=PACK))
         nc.sync.dma_start(offsets[:], offs)
         nc.sync.dma_start(ow_rows[0:P:BLOCK, :], ow[0].rearrange("(b i) o -> b (i o)", i=BLOCK))
         nc.sync.dma_start(r_head[:], r_planes[:, 0:2, :])
-        for t in (2, 3):
-            nc.sync.dma_start(k_win[t], k_planes[:, t, :])
-            nc.sync.dma_start(r_win[t], r_planes[:, t, :])
+        nc.sync.dma_start(r_win2[:], r_planes[:, 2, :])
+        nc.sync.dma_start(r_win3[:], r_planes[:, 3, :])
         nc.sync.dma_start(q_raw[:], qT[0].rearrange("(p t) q -> p t q", t=PACK))
 
         nc.vector.transpose(ow_cols[:], ow_rows[:])
@@ -66,13 +64,13 @@ def tile_attend_pre_diffscat_f_topk_kernel(tc, qT, kT, rT, ow, offs, out):
 
         cols = [slice(c * CHUNK, (c + 1) * CHUNK) for c in range(CHUNKS)]
         k_low = tile([P, 2, N], F32, "k_low")
+        k_high = tile([P, 2, N], F32, "k_high")
         r_low = tile([P, 2, N], F32, "r_low")
-        k_got = {t: tile([P, N], F32, f"k_got{t}") for t in (2, 3)}
-        r_got2 = tile([P, N], F32, "r_got2")
-        r_last = [tile([P, CHUNK], F32, f"r_last{c}") for c in range(3)]
-        r_last.append(shared.tile([P, CHUNK], F32, name="r_last3", align_bytes=256, offset=3 * 4 * CHUNK))
-        u_low = tile([P, 3, N], BF16, "u_low")
-        u_last = tile([P, CHUNK], BF16, "u_last")
+        r_pair = [tile([P, 2, CHUNK], F32, f"r_pair{c}") for c in range(2)]
+        r_mid = tile([P, HALF], F32, "r_mid")
+        r_last2 = tile([P, CHUNK], F32, "r_last2")
+        r_last3 = shared.tile([P, CHUNK], F32, name="r_last3", align_bytes=256, offset=3 * 4 * CHUNK)
+        u_dense = tile([P, 2, CHUNK], BF16, "u_dense")
         u_words = [tile([P, CHUNK, PACK], BF16, f"u_words{c}") for c in range(CHUNKS)]
         u_codes = [
             shared.tile([P, CHUNK], U32, name=f"u_codes{c}", align_bytes=256, offset=4 * c * CHUNK) for c in range(3)
@@ -87,6 +85,12 @@ def tile_attend_pre_diffscat_f_topk_kernel(tc, qT, kT, rT, ow, offs, out):
 
         def listed(first, last):
             return offsets[:, first // LIST_ROWS : last // LIST_ROWS]
+
+        def chunk(c):
+            return listed(c * CHUNK, (c + 1) * CHUNK)
+
+        def slot_major(planes):
+            return planes.rearrange("p t i -> p i t")
 
         def quantize(codes, scales, words):
             nc.vector.quantize_mx(
@@ -104,55 +108,48 @@ def tile_attend_pre_diffscat_f_topk_kernel(tc, qT, kT, rT, ow, offs, out):
                 stop=True,
             )
 
-        def place(c, planes):
-            nc.scalar.copy(u_words[c][:, :, 0:planes], u_low[:, 0:planes, cols[c]].rearrange("p t i -> p i t"))
+        for t, got in ((0, k_low), (2, k_high)):
+            nc.vector.tensor_copy(got[:, 0, :], k_win[:, t, :].indirect(offsets[:]))
+            nc.scalar.activation(got[:, 1, :], k_win[:, t + 1, :].indirect(offsets[:]), COPY)
+        nc.vector.tensor_copy(r_low[:, 0, :], r_head[:, 0, :].indirect(offsets[:]))
+        nc.scalar.activation(r_low[:, 1, :], r_head[:, 1, :].indirect(offsets[:]), COPY)
+        for c in range(CHUNKS):
+            nc.vector.tensor_tensor(
+                u_words[c][:, :, 0:2], slot_major(k_low[:, :, cols[c]]), slot_major(r_low[:, :, cols[c]]), SUB
+            )
+        nc.scalar.activation(r_mid[:], r_win2[:].indirect(listed(HALF, N)), COPY)
+        for c in range(2):
+            nc.scalar.activation(r_pair[c][:, 0, :], r_win2[:].indirect(chunk(c)), COPY)
+        nc.vector.tensor_tensor(u_dense[:, 0, :], k_high[:, 0, cols[2]], r_mid[:, 0:CHUNK], SUB)
+        nc.vector.tensor_tensor(u_words[3][:, :, 2], k_high[:, 0, cols[3]], r_mid[:, CHUNK:HALF], SUB)
 
-        nc.vector.tensor_copy(k_low[:, 0, :], k_win[0].indirect(offsets[:]))
-        nc.scalar.activation(k_low[:, 1, :], k_win[1].indirect(offsets[:]), COPY)
-        nc.vector.tensor_copy(r_low[:, 0, :], r_win[0].indirect(offsets[:]))
-        nc.scalar.activation(r_low[:, 1, :], r_win[1].indirect(offsets[:]), COPY)
-        nc.vector.tensor_tensor(u_low[:, 0:2, :], k_low[:], r_low[:], SUB)
-        nc.vector.tensor_copy(k_got[2][:], k_win[2].indirect(offsets[:]))
-        for c in (0, 1, 3):
-            place(c, 2)
-        nc.vector.tensor_copy(r_got2[:], r_win[2].indirect(offsets[:]))
-        nc.vector.tensor_tensor(u_low[:, 2, cols[2]], k_got[2][:, cols[2]], r_got2[:, cols[2]], SUB)
-        for c in (0, 1, 3):
-            nc.vector.tensor_tensor(u_words[c][:, :, 2], k_got[2][:, cols[c]], r_got2[:, cols[c]], SUB)
-        place(2, 3)
-        nc.scalar.activation(k_got[3][:], k_win[3].indirect(offsets[:]), COPY)
-
-        def gather_last(c):
-            return r_win[3].indirect(listed(c * CHUNK, (c + 1) * CHUNK))
-
-        def subtract_last(c):
-            nc.vector.tensor_tensor(u_words[c][:, :, 3], k_got[3][:, cols[c]], r_last[c][:], SUB)
-
-        for c in (2, 1):
-            nc.vector.tensor_copy(r_last[c][:], gather_last(c))
-        nc.scalar.activation(r_last[0][:], gather_last(0), COPY)
+        nc.vector.tensor_copy(r_last2[:], r_win3[:].indirect(chunk(2)))
+        nc.vector.tensor_copy(r_pair[1][:, 1, :], r_win3[:].indirect(chunk(1)))
+        nc.scalar.activation(r_pair[0][:, 1, :], r_win3[:].indirect(chunk(0)), COPY)
         nc.scalar.copy(
             q_words[:].rearrange("p (c i) t -> p c t i", i=4), q_raw[:].rearrange("p t (c i) -> p c t i", i=4)
         )
-        nc.vector.tensor_tensor(u_last[:], k_got[3][:, cols[2]], r_last[2][:], SUB)
-        nc.scalar.copy(u_words[2][:, :, 3], u_last[:])
-        nc.scalar.activation(r_last[3][:], gather_last(3), COPY)
-        for c in (0, 1):
-            subtract_last(c)
+        nc.vector.tensor_tensor(u_dense[:, 1, :], k_high[:, 1, cols[2]], r_last2[:], SUB)
+        nc.scalar.copy(u_words[2][:, :, 2:4], slot_major(u_dense[:]))
+        nc.scalar.activation(r_last3[:], r_win3[:].indirect(chunk(3)), COPY)
+        for c in range(2):
+            nc.vector.tensor_tensor(
+                u_words[c][:, :, 2:4], slot_major(k_high[:, :, cols[c]]), slot_major(r_pair[c][:]), SUB
+            )
         quantize(u_codes[0], u_scales[0], u_words[0])
         quantize(q_codes, q_scales, q_words)
         for c in (1, 2):
             quantize(u_codes[c], u_scales[c], u_words[c])
-        subtract_last(3)
+        nc.vector.tensor_tensor(u_words[3][:, :, 3], k_high[:, 1, cols[3]], r_last3[:], SUB)
         quantize(u_codes[3], u_scales[3], u_words[3])
         for c in range(CHUNKS):
             multiply(c)
         for c in range(3):
             nc.scalar.activation(y[:, cols[c]], acc[c][:], COPY, scale=ow_col)
-        nc.vector.tensor_tensor(maps[1][:].indirect(listed(0, CHUNK)), y[:, cols[0]], zeros[:], ADD)
+        nc.vector.tensor_tensor(maps[1][:].indirect(chunk(0)), y[:, cols[0]], zeros[:], ADD)
         nc.scalar.activation(maps[0][:].indirect(listed(CHUNK, 3 * CHUNK)), y[:, CHUNK : 3 * CHUNK], COPY)
         nc.vector.tensor_scalar_mul(y[:, cols[3]], acc[3][:], ow_col)
-        nc.vector.tensor_tensor(maps[1][:].indirect(listed(3 * CHUNK, N)), y[:, cols[3]], zeros[:], ADD)
+        nc.vector.tensor_tensor(maps[1][:].indirect(chunk(3)), y[:, cols[3]], zeros[:], ADD)
 
         for n, width in enumerate(PIECES):
             first = sum(PIECES[:n])

@@ -65,12 +65,11 @@ def tile_attend_pre_diffscat_f_topk_kernel(tc, qT, kT, rT, ow, offs, out):
         cols = [slice(c * CHUNK, (c + 1) * CHUNK) for c in range(CHUNKS)]
         k_low = tile([P, 2, N], F32, "k_low")
         k_high = tile([P, 2, N], F32, "k_high")
-        r_low = tile([P, 2, N], F32, "r_low")
-        r_pair = [tile([P, 2, CHUNK], F32, f"r_pair{c}") for c in range(2)]
-        r_mid = tile([P, HALF], F32, "r_mid")
-        r_last2 = tile([P, CHUNK], F32, "r_last2")
-        r_last3 = shared.tile([P, CHUNK], F32, name="r_last3", align_bytes=256, offset=3 * 4 * CHUNK)
-        u_dense = tile([P, 2, CHUNK], BF16, "u_dense")
+        r_low = [tile([P, 2, HALF], F32, f"r_low{h}") for h in range(2)]
+        r_mid = [tile([P, CHUNK], F32, f"r_mid{c}") for c in range(CHUNKS)]
+        r_last = [tile([P, CHUNK], F32, f"r_last{c}") for c in range(3)]
+        r_last.append(shared.tile([P, CHUNK], F32, name="r_last3", align_bytes=256, offset=3 * 4 * CHUNK))
+        u_dense = {t: tile([P, CHUNK], BF16, f"u_dense{t}") for t in (2, 3)}
         u_words = [tile([P, CHUNK, PACK], BF16, f"u_words{c}") for c in range(CHUNKS)]
         u_codes = [
             shared.tile([P, CHUNK], U32, name=f"u_codes{c}", align_bytes=256, offset=4 * c * CHUNK) for c in range(3)
@@ -111,43 +110,47 @@ def tile_attend_pre_diffscat_f_topk_kernel(tc, qT, kT, rT, ow, offs, out):
         for t, got in ((0, k_low), (2, k_high)):
             nc.vector.tensor_copy(got[:, 0, :], k_win[:, t, :].indirect(offsets[:]))
             nc.scalar.activation(got[:, 1, :], k_win[:, t + 1, :].indirect(offsets[:]), COPY)
-        nc.vector.tensor_copy(r_low[:, 0, :], r_head[:, 0, :].indirect(offsets[:]))
-        nc.scalar.activation(r_low[:, 1, :], r_head[:, 1, :].indirect(offsets[:]), COPY)
+        nc.vector.tensor_copy(r_low[0][:, 0, :], r_head[:, 0, :].indirect(listed(0, HALF)))
+        nc.scalar.activation(r_low[0][:, 1, :], r_head[:, 1, :].indirect(listed(0, HALF)), COPY)
+        for t in range(2):
+            nc.scalar.activation(r_low[1][:, t, :], r_head[:, t, :].indirect(listed(HALF, N)), COPY)
         for c in range(CHUNKS):
             nc.vector.tensor_tensor(
-                u_words[c][:, :, 0:2], slot_major(k_low[:, :, cols[c]]), slot_major(r_low[:, :, cols[c]]), SUB
+                u_words[c][:, :, 0:2], slot_major(k_low[:, :, cols[c]]), slot_major(r_low[c // 2][:, :, cols[c % 2]]), SUB
             )
-        nc.scalar.activation(r_mid[:], r_win2[:].indirect(listed(HALF, N)), COPY)
-        for c in range(2):
-            nc.scalar.activation(r_pair[c][:, 0, :], r_win2[:].indirect(chunk(c)), COPY)
-        nc.vector.tensor_tensor(u_dense[:, 0, :], k_high[:, 0, cols[2]], r_mid[:, 0:CHUNK], SUB)
-        nc.vector.tensor_tensor(u_words[3][:, :, 2], k_high[:, 0, cols[3]], r_mid[:, CHUNK:HALF], SUB)
 
-        nc.vector.tensor_copy(r_last2[:], r_win3[:].indirect(chunk(2)))
-        nc.vector.tensor_copy(r_pair[1][:, 1, :], r_win3[:].indirect(chunk(1)))
-        nc.scalar.activation(r_pair[0][:, 1, :], r_win3[:].indirect(chunk(0)), COPY)
+        def subtract(c, t, r_got):
+            into = u_dense[t][:] if c == 2 else u_words[c][:, :, t]
+            nc.vector.tensor_tensor(into, k_high[:, t - 2, cols[c]], r_got[c][:], SUB)
+
+        for c in (0, 2, 1, 3):
+            nc.scalar.activation(r_mid[c][:], r_win2[:].indirect(chunk(c)), COPY)
+            subtract(c, 2, r_mid)
+        nc.scalar.copy(u_words[2][:, :, 2], u_dense[2][:])
+
+        for c in (2, 1):
+            nc.vector.tensor_copy(r_last[c][:], r_win3[:].indirect(chunk(c)))
+        nc.scalar.activation(r_last[0][:], r_win3[:].indirect(chunk(0)), COPY)
         nc.scalar.copy(
             q_words[:].rearrange("p (c i) t -> p c t i", i=4), q_raw[:].rearrange("p t (c i) -> p c t i", i=4)
         )
-        nc.vector.tensor_tensor(u_dense[:, 1, :], k_high[:, 1, cols[2]], r_last2[:], SUB)
-        nc.scalar.copy(u_words[2][:, :, 2:4], slot_major(u_dense[:]))
-        nc.scalar.activation(r_last3[:], r_win3[:].indirect(chunk(3)), COPY)
+        subtract(2, 3, r_last)
+        nc.scalar.copy(u_words[2][:, :, 3], u_dense[3][:])
+        nc.scalar.activation(r_last[3][:], r_win3[:].indirect(chunk(3)), COPY)
         for c in range(2):
-            nc.vector.tensor_tensor(
-                u_words[c][:, :, 2:4], slot_major(k_high[:, :, cols[c]]), slot_major(r_pair[c][:]), SUB
-            )
-        quantize(u_codes[0], u_scales[0], u_words[0])
+            subtract(c, 3, r_last)
         quantize(q_codes, q_scales, q_words)
-        for c in (1, 2):
+        for c in range(3):
             quantize(u_codes[c], u_scales[c], u_words[c])
-        nc.vector.tensor_tensor(u_words[3][:, :, 3], k_high[:, 1, cols[3]], r_last3[:], SUB)
+        subtract(3, 3, r_last)
         quantize(u_codes[3], u_scales[3], u_words[3])
         for c in range(CHUNKS):
             multiply(c)
-        for c in range(3):
-            nc.scalar.activation(y[:, cols[c]], acc[c][:], COPY, scale=ow_col)
+        nc.scalar.activation(y[:, cols[0]], acc[0][:], COPY, scale=ow_col)
+        for c in (1, 2):
+            nc.scalar.copy(y[:, cols[c]], acc[c][:])
         nc.vector.tensor_tensor(maps[1][:].indirect(chunk(0)), y[:, cols[0]], zeros[:], ADD)
-        nc.scalar.activation(maps[0][:].indirect(listed(CHUNK, 3 * CHUNK)), y[:, CHUNK : 3 * CHUNK], COPY)
+        nc.scalar.activation(maps[0][:].indirect(listed(CHUNK, 3 * CHUNK)), y[:, CHUNK : 3 * CHUNK], COPY, scale=ow_col)
         nc.vector.tensor_scalar_mul(y[:, cols[3]], acc[3][:], ow_col)
         nc.vector.tensor_tensor(maps[1][:].indirect(chunk(3)), y[:, cols[3]], zeros[:], ADD)
 

@@ -66,9 +66,12 @@ def tile_attend_pre_diffscat_f_topk_kernel(tc, qT, kT, rT, ow, offs, out):
         k_low = tile([P, 2, N], F32, "k_low")
         k_high = tile([P, 2, N], F32, "k_high")
         r_low = [tile([P, 2, HALF], F32, f"r_low{h}") for h in range(2)]
-        r_mid = [tile([P, CHUNK], F32, f"r_mid{c}") for c in range(CHUNKS)]
-        r_last = [tile([P, CHUNK], F32, f"r_last{c}") for c in range(3)]
-        r_last.append(shared.tile([P, CHUNK], F32, name="r_last3", align_bytes=256, offset=3 * 4 * CHUNK))
+        r_pair = tile([P, 2, CHUNK], F32, "r_pair")
+        r_mid = {c: tile([P, CHUNK], F32, f"r_mid{c}")[:] for c in (0, 2, 3)}
+        r_last = {c: tile([P, CHUNK], F32, f"r_last{c}")[:] for c in (0, 2)}
+        r_mid[1], r_last[1] = r_pair[:, 0, :], r_pair[:, 1, :]
+        r_last3 = shared.tile([P, CHUNK], F32, name="r_last3", align_bytes=256, offset=3 * 4 * CHUNK)
+        r_last[3] = r_last3[:]
         u_dense = {t: tile([P, CHUNK], BF16, f"u_dense{t}") for t in (2, 3)}
         u_words = [tile([P, CHUNK, PACK], BF16, f"u_words{c}") for c in range(CHUNKS)]
         u_codes = [
@@ -121,32 +124,34 @@ def tile_attend_pre_diffscat_f_topk_kernel(tc, qT, kT, rT, ow, offs, out):
 
         def subtract(c, t, r_got):
             into = u_dense[t][:] if c == 2 else u_words[c][:, :, t]
-            nc.vector.tensor_tensor(into, k_high[:, t - 2, cols[c]], r_got[c][:], SUB)
+            nc.vector.tensor_tensor(into, k_high[:, t - 2, cols[c]], r_got[c], SUB)
 
-        for c in (0, 2, 1, 3):
-            nc.scalar.activation(r_mid[c][:], r_win2[:].indirect(chunk(c)), COPY)
+        for c in (0, 2, 3):
+            nc.scalar.activation(r_mid[c], r_win2[:].indirect(chunk(c)), COPY)
             subtract(c, 2, r_mid)
+        nc.scalar.activation(r_mid[1], r_win2[:].indirect(chunk(1)), COPY)
         nc.scalar.copy(u_words[2][:, :, 2], u_dense[2][:])
 
         for c in (2, 1):
-            nc.vector.tensor_copy(r_last[c][:], r_win3[:].indirect(chunk(c)))
-        nc.scalar.activation(r_last[0][:], r_win3[:].indirect(chunk(0)), COPY)
+            nc.vector.tensor_copy(r_last[c], r_win3[:].indirect(chunk(c)))
+        nc.scalar.activation(r_last[0], r_win3[:].indirect(chunk(0)), COPY)
         nc.scalar.copy(
             q_words[:].rearrange("p (c i) t -> p c t i", i=4), q_raw[:].rearrange("p t (c i) -> p c t i", i=4)
         )
         subtract(2, 3, r_last)
         nc.scalar.copy(u_words[2][:, :, 3], u_dense[3][:])
-        nc.scalar.activation(r_last[3][:], r_win3[:].indirect(chunk(3)), COPY)
-        for c in range(2):
-            subtract(c, 3, r_last)
+        nc.scalar.activation(r_last[3], r_win3[:].indirect(chunk(3)), COPY)
+        subtract(0, 3, r_last)
+        nc.vector.tensor_tensor(u_words[1][:, :, 2:4], slot_major(k_high[:, :, cols[1]]), slot_major(r_pair[:]), SUB)
         quantize(q_codes, q_scales, q_words)
         for c in range(3):
             quantize(u_codes[c], u_scales[c], u_words[c])
-        subtract(3, 3, r_last)
-        quantize(u_codes[3], u_scales[3], u_words[3])
-        for c in range(CHUNKS):
+        for c in range(3):
             multiply(c)
-        nc.scalar.activation(y[:, cols[0]], acc[0][:], COPY, scale=ow_col)
+        subtract(3, 3, r_last)
+        nc.vector.tensor_scalar_mul(y[:, cols[0]], acc[0][:], ow_col)
+        quantize(u_codes[3], u_scales[3], u_words[3])
+        multiply(3)
         for c in (1, 2):
             nc.scalar.copy(y[:, cols[c]], acc[c][:])
         nc.vector.tensor_tensor(maps[1][:].indirect(chunk(0)), y[:, cols[0]], zeros[:], ADD)

@@ -22,6 +22,7 @@ CHUNK = 128
 CHUNKS = N // CHUNK
 HALF = N // 2
 BLOCK = 32
+FIRST = 96
 PIECES = (192, 256, 320, 384, 448, 448)
 
 
@@ -149,13 +150,14 @@ def tile_attend_pre_diffscat_f_topk_kernel(tc, qT, kT, rT, ow, offs, out):
         for c in range(3):
             multiply(c)
         subtract(3, 3, r_last)
-        nc.vector.tensor_scalar_mul(y[:, cols[0]], acc[0][:], ow_col)
+        nc.vector.tensor_scalar_mul(y[:, 0:FIRST], acc[0][:, 0:FIRST], ow_col)
+        nc.scalar.copy(y[:, FIRST:CHUNK], acc[0][:, FIRST:CHUNK])
         quantize(u_codes[3], u_scales[3], u_words[3])
         multiply(3)
         for c in (1, 2):
             nc.scalar.copy(y[:, cols[c]], acc[c][:])
-        nc.vector.tensor_tensor(maps[1][:].indirect(chunk(0)), y[:, cols[0]], zeros[:], ADD)
-        nc.scalar.activation(maps[0][:].indirect(listed(CHUNK, 3 * CHUNK)), y[:, CHUNK : 3 * CHUNK], COPY, scale=ow_col)
+        nc.vector.tensor_tensor(maps[1][:].indirect(listed(0, FIRST)), y[:, 0:FIRST], zeros[:, 0:FIRST], ADD)
+        nc.scalar.activation(maps[0][:].indirect(listed(FIRST, 3 * CHUNK)), y[:, FIRST : 3 * CHUNK], COPY, scale=ow_col)
         nc.vector.tensor_scalar_mul(y[:, cols[3]], acc[3][:], ow_col)
         nc.vector.tensor_tensor(maps[1][:].indirect(chunk(3)), y[:, cols[3]], zeros[:], ADD)
 

@@ -151,7 +151,7 @@ def tile_attend_pre_diffscat_f_topk_kernel(tc, qT, kT, rT, ow, offs, out):
             multiply(c)
         subtract(3, 3, r_last)
         nc.vector.tensor_scalar_mul(y[:, 0:FIRST], acc[0][:, 0:FIRST], ow_col)
-        nc.scalar.copy(y[:, FIRST:CHUNK], acc[0][:, FIRST:CHUNK])
+        nc.vector.tensor_copy(y[:, FIRST:CHUNK], acc[0][:, FIRST:CHUNK])
         quantize(u_codes[3], u_scales[3], u_words[3])
         multiply(3)
         for c in (1, 2):

@@ -43,38 +43,36 @@ def tile_attend_pre_diffscat_f_topk_kernel(tc, qT, kT, rT, ow, offs, out):
         r_win2 = tile([P, T], F32, "r_win2")
         r_win3 = tile([P, T], F32, "r_win3")
         q_raw = shared.tile([P, PACK, NQ], F32, name="q_raw", align_bytes=256, offset=0)
-        ow_rows = tile([P, BLOCK], F32, "ow_rows")
+        cleared = tile([P, CHUNK + BLOCK], F32, "cleared")
+        zeros, ow_rows = cleared[:, 0:CHUNK], cleared[:, CHUNK : CHUNK + BLOCK]
         ow_cols = tile([P, BLOCK], F32, "ow_cols")
         ow_col = ow_cols[:, 0:1]
-        nc.vector.memset(ow_rows[:], 0.0)
+        nc.vector.memset(cleared[:], 0.0)
 
         nc.sync.dma_start(k_win[:], kT.rearrange("(p t) c -> p t c", t=PACK))
         nc.sync.dma_start(offsets[:], offs)
-        nc.sync.dma_start(ow_rows[0:P:BLOCK, :], ow[0].rearrange("(b i) o -> b (i o)", i=BLOCK))
+        nc.sync.dma_start(cleared[0:P:BLOCK, CHUNK : CHUNK + BLOCK], ow[0].rearrange("(b i) o -> b (i o)", i=BLOCK))
         nc.sync.dma_start(r_head[:], r_planes[:, 0:2, :])
         nc.sync.dma_start(r_win2[:], r_planes[:, 2, :])
         nc.sync.dma_start(r_win3[:], r_planes[:, 3, :])
         nc.sync.dma_start(q_raw[:], qT[0].rearrange("(p t) q -> p t q", t=PACK))
 
-        nc.vector.transpose(ow_cols[:], ow_rows[:])
+        nc.vector.transpose(ow_cols[:], ow_rows)
         maps = [tile([P, T], F32, f"map{h}") for h in range(2)]
         for h in range(2):
             nc.vector.memset(maps[h][:], 0.0)
-        zeros = tile([P, CHUNK], F32, "zeros")
-        nc.vector.memset(zeros[:], 0.0)
 
         cols = [slice(c * CHUNK, (c + 1) * CHUNK) for c in range(CHUNKS)]
         k_low = tile([P, 2, N], F32, "k_low")
         k_high = tile([P, 2, N], F32, "k_high")
-        r_low = [tile([P, 2, HALF], F32, f"r_low{h}") for h in range(2)]
-        r_pair = tile([P, 2, CHUNK], F32, "r_pair")
-        r_mid = {c: tile([P, CHUNK], F32, f"r_mid{c}")[:] for c in (0, 2, 3)}
-        r_last = {c: tile([P, CHUNK], F32, f"r_last{c}")[:] for c in (0, 2)}
-        r_mid[1], r_last[1] = r_pair[:, 0, :], r_pair[:, 1, :]
+        r_low = tile([P, 2, N], F32, "r_low")
+        r_pairs = tile([P, 2, HALF], F32, "r_pairs")
+        r_mid = tile([P, HALF], F32, "r_mid")
+        r_last2 = tile([P, CHUNK], F32, "r_last2")
         r_last3 = shared.tile([P, CHUNK], F32, name="r_last3", align_bytes=256, offset=3 * 4 * CHUNK)
-        r_last[3] = r_last3[:]
-        u_dense = {t: tile([P, CHUNK], BF16, f"u_dense{t}") for t in (2, 3)}
-        u_words = [tile([P, CHUNK, PACK], BF16, f"u_words{c}") for c in range(CHUNKS)]
+        u_dense = tile([P, 2, CHUNK], BF16, "u_dense")
+        u_halves = [tile([P, HALF, PACK], BF16, f"u_half{h}") for h in range(2)]
+        u_words = [u_halves[c // 2][:, cols[c % 2], :] for c in range(CHUNKS)]
         u_codes = [
             shared.tile([P, CHUNK], U32, name=f"u_codes{c}", align_bytes=256, offset=4 * c * CHUNK) for c in range(3)
         ]
@@ -97,7 +95,7 @@ def tile_attend_pre_diffscat_f_topk_kernel(tc, qT, kT, rT, ow, offs, out):
 
         def quantize(codes, scales, words):
             nc.vector.quantize_mx(
-                out=codes[:].bitcast(FP8X4), scales=scales[:], in_=words[:].rearrange("p i t -> p (i t)")
+                out=codes[:].bitcast(FP8X4), scales=scales[:], in_=words.rearrange("p i t -> p (i t)")
             )
 
         def multiply(c):
@@ -114,52 +112,47 @@ def tile_attend_pre_diffscat_f_topk_kernel(tc, qT, kT, rT, ow, offs, out):
         for t, got in ((0, k_low), (2, k_high)):
             nc.vector.tensor_copy(got[:, 0, :], k_win[:, t, :].indirect(offsets[:]))
             nc.scalar.activation(got[:, 1, :], k_win[:, t + 1, :].indirect(offsets[:]), COPY)
-        nc.vector.tensor_copy(r_low[0][:, 0, :], r_head[:, 0, :].indirect(listed(0, HALF)))
-        nc.scalar.activation(r_low[0][:, 1, :], r_head[:, 1, :].indirect(listed(0, HALF)), COPY)
-        for t in range(2):
-            nc.scalar.activation(r_low[1][:, t, :], r_head[:, t, :].indirect(listed(HALF, N)), COPY)
-        for c in range(CHUNKS):
+        nc.vector.tensor_copy(r_low[:, 0, :], r_head[:, 0, :].indirect(offsets[:]))
+        nc.scalar.activation(r_low[:, 1, :], r_head[:, 1, :].indirect(offsets[:]), COPY)
+        for h in range(2):
+            half = slice(h * HALF, (h + 1) * HALF)
             nc.vector.tensor_tensor(
-                u_words[c][:, :, 0:2], slot_major(k_low[:, :, cols[c]]), slot_major(r_low[c // 2][:, :, cols[c % 2]]), SUB
+                u_halves[h][:, :, 0:2], slot_major(k_low[:, :, half]), slot_major(r_low[:, :, half]), SUB
             )
+        nc.scalar.activation(r_mid[:], r_win2[:].indirect(listed(HALF, N)), COPY)
+        nc.scalar.activation(r_pairs[:, 0, :], r_win2[:].indirect(listed(0, HALF)), COPY)
+        nc.vector.tensor_tensor(u_dense[:, 0, :], k_high[:, 0, cols[2]], r_mid[:, cols[0]], SUB)
+        nc.vector.tensor_tensor(u_words[3][:, :, 2], k_high[:, 0, cols[3]], r_mid[:, cols[1]], SUB)
 
-        def subtract(c, t, r_got):
-            into = u_dense[t][:] if c == 2 else u_words[c][:, :, t]
-            nc.vector.tensor_tensor(into, k_high[:, t - 2, cols[c]], r_got[c], SUB)
-
-        for c in (0, 2, 3):
-            nc.scalar.activation(r_mid[c], r_win2[:].indirect(chunk(c)), COPY)
-            subtract(c, 2, r_mid)
-        nc.scalar.activation(r_mid[1], r_win2[:].indirect(chunk(1)), COPY)
-        nc.scalar.copy(u_words[2][:, :, 2], u_dense[2][:])
-
-        for c in (2, 1):
-            nc.vector.tensor_copy(r_last[c], r_win3[:].indirect(chunk(c)))
-        nc.scalar.activation(r_last[0], r_win3[:].indirect(chunk(0)), COPY)
+        nc.vector.tensor_copy(r_last2[:], r_win3[:].indirect(chunk(2)))
+        nc.vector.tensor_copy(r_pairs[:, 1, cols[1]], r_win3[:].indirect(chunk(1)))
+        nc.scalar.activation(r_pairs[:, 1, cols[0]], r_win3[:].indirect(chunk(0)), COPY)
         nc.scalar.copy(
             q_words[:].rearrange("p (c i) t -> p c t i", i=4), q_raw[:].rearrange("p t (c i) -> p c t i", i=4)
         )
-        subtract(2, 3, r_last)
-        nc.scalar.copy(u_words[2][:, :, 3], u_dense[3][:])
-        nc.scalar.activation(r_last[3], r_win3[:].indirect(chunk(3)), COPY)
-        subtract(0, 3, r_last)
-        nc.vector.tensor_tensor(u_words[1][:, :, 2:4], slot_major(k_high[:, :, cols[1]]), slot_major(r_pair[:]), SUB)
-        quantize(q_codes, q_scales, q_words)
+        nc.vector.tensor_tensor(u_dense[:, 1, :], k_high[:, 1, cols[2]], r_last2[:], SUB)
+        nc.scalar.copy(u_words[2][:, :, 2:4], slot_major(u_dense[:]))
+        nc.scalar.activation(r_last3[:], r_win3[:].indirect(chunk(3)), COPY)
+        for c in range(2):
+            nc.vector.tensor_tensor(
+                u_words[c][:, :, 2:4], slot_major(k_high[:, :, cols[c]]), slot_major(r_pairs[:, :, cols[c]]), SUB
+            )
+        quantize(q_codes, q_scales, q_words[:])
         for c in range(3):
             quantize(u_codes[c], u_scales[c], u_words[c])
         for c in range(3):
             multiply(c)
-        subtract(3, 3, r_last)
+        nc.vector.tensor_tensor(u_words[3][:, :, 3], k_high[:, 1, cols[3]], r_last3[:], SUB)
         nc.vector.tensor_scalar_mul(y[:, 0:FIRST], acc[0][:, 0:FIRST], ow_col)
         nc.vector.tensor_copy(y[:, FIRST:CHUNK], acc[0][:, FIRST:CHUNK])
         quantize(u_codes[3], u_scales[3], u_words[3])
         multiply(3)
         for c in (1, 2):
             nc.scalar.copy(y[:, cols[c]], acc[c][:])
-        nc.vector.tensor_tensor(maps[1][:].indirect(listed(0, FIRST)), y[:, 0:FIRST], zeros[:, 0:FIRST], ADD)
+        nc.vector.tensor_tensor(maps[1][:].indirect(listed(0, FIRST)), y[:, 0:FIRST], cleared[:, 0:FIRST], ADD)
         nc.scalar.activation(maps[0][:].indirect(listed(FIRST, 3 * CHUNK)), y[:, FIRST : 3 * CHUNK], COPY, scale=ow_col)
         nc.vector.tensor_scalar_mul(y[:, cols[3]], acc[3][:], ow_col)
-        nc.vector.tensor_tensor(maps[1][:].indirect(chunk(3)), y[:, cols[3]], zeros[:], ADD)
+        nc.vector.tensor_tensor(maps[1][:].indirect(chunk(3)), y[:, cols[3]], zeros, ADD)
 
         for n, width in enumerate(PIECES):
             first = sum(PIECES[:n])

@@ -19,10 +19,10 @@ P = 128
 PACK = 4
 LIST_ROWS = 16
 CHUNK = 128
-CHUNKS = N // CHUNK
-HALF = N // 2
 BLOCK = 32
-FIRST = 96
+EDGES = (0, 64, 192, 320, 448, 512)
+ZEROS = 192
+CHUNKS = len(EDGES) - 1
 PIECES = (192, 256, 320, 384, 448, 448)
 
 
@@ -43,15 +43,15 @@ def tile_attend_pre_diffscat_f_topk_kernel(tc, qT, kT, rT, ow, offs, out):
         r_win2 = tile([P, T], F32, "r_win2")
         r_win3 = tile([P, T], F32, "r_win3")
         q_raw = shared.tile([P, PACK, NQ], F32, name="q_raw", align_bytes=256, offset=0)
-        cleared = tile([P, CHUNK + BLOCK], F32, "cleared")
-        zeros, ow_rows = cleared[:, 0:CHUNK], cleared[:, CHUNK : CHUNK + BLOCK]
+        cleared = tile([P, ZEROS + BLOCK], F32, "cleared")
+        ow_rows = cleared[:, ZEROS : ZEROS + BLOCK]
         ow_cols = tile([P, BLOCK], F32, "ow_cols")
         ow_col = ow_cols[:, 0:1]
         nc.vector.memset(cleared[:], 0.0)
 
         nc.sync.dma_start(k_win[:], kT.rearrange("(p t) c -> p t c", t=PACK))
         nc.sync.dma_start(offsets[:], offs)
-        nc.sync.dma_start(cleared[0:P:BLOCK, CHUNK : CHUNK + BLOCK], ow[0].rearrange("(b i) o -> b (i o)", i=BLOCK))
+        nc.sync.dma_start(cleared[0:P:BLOCK, ZEROS : ZEROS + BLOCK], ow[0].rearrange("(b i) o -> b (i o)", i=BLOCK))
         nc.sync.dma_start(r_head[:], r_planes[:, 0:2, :])
         nc.sync.dma_start(r_win2[:], r_planes[:, 2, :])
         nc.sync.dma_start(r_win3[:], r_planes[:, 3, :])
@@ -62,33 +62,33 @@ def tile_attend_pre_diffscat_f_topk_kernel(tc, qT, kT, rT, ow, offs, out):
         for h in range(2):
             nc.vector.memset(maps[h][:], 0.0)
 
-        cols = [slice(c * CHUNK, (c + 1) * CHUNK) for c in range(CHUNKS)]
+        cols = [slice(EDGES[c], EDGES[c + 1]) for c in range(CHUNKS)]
+        wide = [EDGES[c + 1] - EDGES[c] for c in range(CHUNKS)]
         k_low = tile([P, 2, N], F32, "k_low")
         k_high = tile([P, 2, N], F32, "k_high")
         r_low = tile([P, 2, N], F32, "r_low")
-        r_pairs = tile([P, 2, HALF], F32, "r_pairs")
-        r_mid = tile([P, HALF], F32, "r_mid")
-        r_last2 = tile([P, CHUNK], F32, "r_last2")
-        r_last3 = shared.tile([P, CHUNK], F32, name="r_last3", align_bytes=256, offset=3 * 4 * CHUNK)
-        u_dense = tile([P, 2, CHUNK], BF16, "u_dense")
-        u_halves = [tile([P, HALF, PACK], BF16, f"u_half{h}") for h in range(2)]
-        u_words = [u_halves[c // 2][:, cols[c % 2], :] for c in range(CHUNKS)]
+        r_pairs = tile([P, 2, EDGES[2]], F32, "r_pairs")
+        r_mid = tile([P, N - EDGES[2]], F32, "r_mid")
+        r_last = {c: tile([P, CHUNK], F32, f"r_last{c}") for c in (2, 3)}
+        r_last4 = shared.tile([P, wide[4]], F32, name="r_last4", align_bytes=256, offset=3 * 4 * CHUNK)
+        u_dense = tile([P, 2, 2 * CHUNK], BF16, "u_dense")
+        u_words = tile([P, N, PACK], BF16, "u_words")
         u_codes = [
-            shared.tile([P, CHUNK], U32, name=f"u_codes{c}", align_bytes=256, offset=4 * c * CHUNK) for c in range(3)
+            shared.tile([P, wide[c]], U32, name=f"u_codes{c}", align_bytes=256, offset=4 * c * CHUNK) for c in range(3)
         ]
-        u_codes.append(tile([P, CHUNK], U32, "u_codes3"))
-        u_scales = [tile([P, CHUNK], U8, f"u_scales{c}") for c in range(CHUNKS)]
+        u_codes.extend(tile([P, wide[c]], U32, f"u_codes{c}") for c in (3, 4))
+        u_scales = [tile([P, wide[c]], U8, f"u_scales{c}") for c in range(CHUNKS)]
         q_words = tile([P, NQ, PACK], BF16, "q_words")
         q_codes = tile([P, NQ], U32, "q_codes")
         q_scales = tile([P, NQ], U8, "q_scales")
-        acc = [psum.tile([NQ, CHUNK], F32, name=f"acc{c}") for c in range(CHUNKS)]
+        acc = [psum.tile([NQ, wide[c]], F32, name=f"acc{c}") for c in range(CHUNKS)]
         y = tile([NQ, N], F32, "y")
 
         def listed(first, last):
             return offsets[:, first // LIST_ROWS : last // LIST_ROWS]
 
         def chunk(c):
-            return listed(c * CHUNK, (c + 1) * CHUNK)
+            return listed(EDGES[c], EDGES[c + 1])
 
         def slot_major(planes):
             return planes.rearrange("p t i -> p i t")
@@ -98,7 +98,8 @@ def tile_attend_pre_diffscat_f_topk_kernel(tc, qT, kT, rT, ow, offs, out):
                 out=codes[:].bitcast(FP8X4), scales=scales[:], in_=words.rearrange("p i t -> p (i t)")
             )
 
-        def multiply(c):
+        def product(c):
+            quantize(u_codes[c], u_scales[c], u_words[:, cols[c], :])
             nc.tensor.matmul_mx(
                 out=acc[c][:],
                 lhsT=q_codes[:].bitcast(FP8X4),
@@ -109,50 +110,66 @@ def tile_attend_pre_diffscat_f_topk_kernel(tc, qT, kT, rT, ow, offs, out):
                 stop=True,
             )
 
+        def dense_cols(c):
+            return slice(EDGES[c] - EDGES[2], EDGES[c + 1] - EDGES[2])
+
+        def subtract_pair(c):
+            nc.vector.tensor_tensor(
+                u_words[:, cols[c], 2:4], slot_major(k_high[:, :, cols[c]]), slot_major(r_pairs[:, :, cols[c]]), SUB
+            )
+
+        def subtract_dense(c):
+            nc.vector.tensor_tensor(u_dense[:, 1, dense_cols(c)], k_high[:, 1, cols[c]], r_last[c][:], SUB)
+
+        def place(c):
+            nc.scalar.copy(u_words[:, cols[c], 2:4], slot_major(u_dense[:, :, dense_cols(c)]))
+
+        def scatter_on_vector(first, last):
+            nc.vector.tensor_tensor(
+                maps[1][:].indirect(listed(first, last)), y[:, first:last], cleared[:, 0 : last - first], ADD
+            )
+
         for t, got in ((0, k_low), (2, k_high)):
             nc.vector.tensor_copy(got[:, 0, :], k_win[:, t, :].indirect(offsets[:]))
             nc.scalar.activation(got[:, 1, :], k_win[:, t + 1, :].indirect(offsets[:]), COPY)
         nc.vector.tensor_copy(r_low[:, 0, :], r_head[:, 0, :].indirect(offsets[:]))
         nc.scalar.activation(r_low[:, 1, :], r_head[:, 1, :].indirect(offsets[:]), COPY)
-        for h in range(2):
-            half = slice(h * HALF, (h + 1) * HALF)
-            nc.vector.tensor_tensor(
-                u_halves[h][:, :, 0:2], slot_major(k_low[:, :, half]), slot_major(r_low[:, :, half]), SUB
-            )
-        nc.scalar.activation(r_mid[:], r_win2[:].indirect(listed(HALF, N)), COPY)
-        nc.scalar.activation(r_pairs[:, 0, :], r_win2[:].indirect(listed(0, HALF)), COPY)
-        nc.vector.tensor_tensor(u_dense[:, 0, :], k_high[:, 0, cols[2]], r_mid[:, cols[0]], SUB)
-        nc.vector.tensor_tensor(u_words[3][:, :, 2], k_high[:, 0, cols[3]], r_mid[:, cols[1]], SUB)
+        nc.vector.tensor_tensor(u_words[:, :, 0:2], slot_major(k_low[:]), slot_major(r_low[:]), SUB)
+        nc.scalar.activation(r_mid[:], r_win2[:].indirect(listed(EDGES[2], N)), COPY)
+        nc.scalar.activation(r_pairs[:, 0, :], r_win2[:].indirect(listed(0, EDGES[2])), COPY)
+        nc.vector.tensor_tensor(u_dense[:, 0, :], k_high[:, 0, EDGES[2] : EDGES[4]], r_mid[:, 0 : 2 * CHUNK], SUB)
+        nc.vector.tensor_tensor(u_words[:, cols[4], 2], k_high[:, 0, cols[4]], r_mid[:, dense_cols(4)], SUB)
 
-        nc.vector.tensor_copy(r_last2[:], r_win3[:].indirect(chunk(2)))
+        nc.vector.tensor_copy(r_last[2][:], r_win3[:].indirect(chunk(2)))
         nc.vector.tensor_copy(r_pairs[:, 1, cols[1]], r_win3[:].indirect(chunk(1)))
         nc.scalar.activation(r_pairs[:, 1, cols[0]], r_win3[:].indirect(chunk(0)), COPY)
+        nc.scalar.activation(r_last[3][:], r_win3[:].indirect(chunk(3)), COPY)
         nc.scalar.copy(
             q_words[:].rearrange("p (c i) t -> p c t i", i=4), q_raw[:].rearrange("p t (c i) -> p c t i", i=4)
         )
-        nc.vector.tensor_tensor(u_dense[:, 1, :], k_high[:, 1, cols[2]], r_last2[:], SUB)
-        nc.scalar.copy(u_words[2][:, :, 2:4], slot_major(u_dense[:]))
-        nc.scalar.activation(r_last3[:], r_win3[:].indirect(chunk(3)), COPY)
-        for c in range(2):
-            nc.vector.tensor_tensor(
-                u_words[c][:, :, 2:4], slot_major(k_high[:, :, cols[c]]), slot_major(r_pairs[:, :, cols[c]]), SUB
-            )
+        subtract_dense(2)
+        subtract_pair(0)
+        subtract_dense(3)
+        subtract_pair(1)
+        place(2)
+        nc.scalar.activation(r_last4[:], r_win3[:].indirect(chunk(4)), COPY)
+        place(3)
         quantize(q_codes, q_scales, q_words[:])
         for c in range(3):
-            quantize(u_codes[c], u_scales[c], u_words[c])
-        for c in range(3):
-            multiply(c)
-        nc.vector.tensor_tensor(u_words[3][:, :, 3], k_high[:, 1, cols[3]], r_last3[:], SUB)
-        nc.vector.tensor_scalar_mul(y[:, 0:FIRST], acc[0][:, 0:FIRST], ow_col)
-        nc.vector.tensor_copy(y[:, FIRST:CHUNK], acc[0][:, FIRST:CHUNK])
-        quantize(u_codes[3], u_scales[3], u_words[3])
-        multiply(3)
+            product(c)
+        nc.vector.tensor_tensor(u_words[:, cols[4], 3], k_high[:, 1, cols[4]], r_last4[:], SUB)
+        for c in (3, 4):
+            product(c)
+        nc.scalar.activation(y[:, cols[0]], acc[0][:], COPY, scale=ow_col)
         for c in (1, 2):
             nc.scalar.copy(y[:, cols[c]], acc[c][:])
-        nc.vector.tensor_tensor(maps[1][:].indirect(listed(0, FIRST)), y[:, 0:FIRST], cleared[:, 0:FIRST], ADD)
-        nc.scalar.activation(maps[0][:].indirect(listed(FIRST, 3 * CHUNK)), y[:, FIRST : 3 * CHUNK], COPY, scale=ow_col)
-        nc.vector.tensor_scalar_mul(y[:, cols[3]], acc[3][:], ow_col)
-        nc.vector.tensor_tensor(maps[1][:].indirect(chunk(3)), y[:, cols[3]], zeros, ADD)
+        scatter_on_vector(0, EDGES[1])
+        nc.scalar.activation(
+            maps[0][:].indirect(listed(EDGES[1], EDGES[3])), y[:, EDGES[1] : EDGES[3]], COPY, scale=ow_col
+        )
+        for c in (3, 4):
+            nc.vector.tensor_scalar_mul(y[:, cols[c]], acc[c][:], ow_col)
+        scatter_on_vector(EDGES[3], N)
 
         for n, width in enumerate(PIECES):
             first = sum(PIECES[:n])

from contextlib import ExitStack

import concourse.mybir as mybir

N, T, D, NQ = 512, 2048, 512, 128
FLOPS = 2 * D * NQ * N

F32 = mybir.dt.float32
BF16 = mybir.dt.bfloat16
U32 = mybir.dt.uint32
U16 = mybir.dt.uint16
U8 = mybir.dt.uint8
FP8X4 = mybir.dt.float8_e4m3fn_x4
COPY = mybir.ActivationFunctionType.Copy
SUB = mybir.AluOpType.subtract
ADD = mybir.AluOpType.add

P = 128
PACK = 4
LIST_ROWS = 16
CHUNK = 128
BLOCK = 32
EDGES = (0, 64, 192, 320, 448, 512)
ZEROS = 192
CHUNKS = len(EDGES) - 1
PIECES = (192, 256, 320, 384, 448, 448)


def tile_attend_pre_diffscat_f_topk_kernel(tc, qT, kT, rT, ow, offs, out):
    nc = tc.nc
    with ExitStack() as ctx:
        keep = ctx.enter_context(tc.tile_pool(name="keep", bufs=1))
        shared = ctx.enter_context(tc.tile_pool(name="shared", bufs=1))
        psum = ctx.enter_context(tc.psum_pool(name="psum", bufs=1))

        def tile(shape, dtype, name):
            return keep.tile(shape, dtype, name=name, align_bytes=256)

        offsets = keep.tile([P, N // LIST_ROWS], U16, name="offsets")
        r_planes = rT.rearrange("(p t) c -> p t c", t=PACK)
        k_win = tile([P, PACK, T], F32, "k_win")
        r_head = tile([P, 2, T], F32, "r_head")
        r_win2 = tile([P, T], F32, "r_win2")
        r_win3 = tile([P, T], F32, "r_win3")
        q_raw = shared.tile([P, PACK, NQ], F32, name="q_raw", align_bytes=256, offset=0)
        cleared = tile([P, ZEROS + BLOCK], F32, "cleared")
        ow_rows = cleared[:, ZEROS : ZEROS + BLOCK]
        ow_cols = tile([P, BLOCK], F32, "ow_cols")
        ow_col = ow_cols[:, 0:1]
        nc.vector.memset(cleared[:], 0.0)

        nc.sync.dma_start(k_win[:], kT.rearrange("(p t) c -> p t c", t=PACK))
        nc.sync.dma_start(offsets[:], offs)
        nc.sync.dma_start(cleared[0:P:BLOCK, ZEROS : ZEROS + BLOCK], ow[0].rearrange("(b i) o -> b (i o)", i=BLOCK))
        nc.sync.dma_start(r_head[:], r_planes[:, 0:2, :])
        nc.sync.dma_start(r_win2[:], r_planes[:, 2, :])
        nc.sync.dma_start(r_win3[:], r_planes[:, 3, :])
        nc.sync.dma_start(q_raw[:], qT[0].rearrange("(p t) q -> p t q", t=PACK))

        nc.vector.transpose(ow_cols[:], ow_rows)
        maps = [tile([P, T], F32, f"map{h}") for h in range(2)]
        for h in range(2):
            nc.vector.memset(maps[h][:], 0.0)

        cols = [slice(EDGES[c], EDGES[c + 1]) for c in range(CHUNKS)]
        wide = [EDGES[c + 1] - EDGES[c] for c in range(CHUNKS)]
        k_low = tile([P, 2, N], F32, "k_low")
        k_high = tile([P, 2, N], F32, "k_high")
        r_low = tile([P, 2, N], F32, "r_low")
        r_pairs = tile([P, 2, EDGES[2]], F32, "r_pairs")
        r_mid = tile([P, N - EDGES[2]], F32, "r_mid")
        r_last = {c: tile([P, CHUNK], F32, f"r_last{c}") for c in (2, 3)}
        r_last4 = shared.tile([P, wide[4]], F32, name="r_last4", align_bytes=256, offset=3 * 4 * CHUNK)
        u_dense = tile([P, 2, 2 * CHUNK], BF16, "u_dense")
        u_words = tile([P, N, PACK], BF16, "u_words")
        u_codes = [
            shared.tile([P, wide[c]], U32, name=f"u_codes{c}", align_bytes=256, offset=4 * c * CHUNK) for c in range(3)
        ]
        u_codes.extend(tile([P, wide[c]], U32, f"u_codes{c}") for c in (3, 4))
        u_scales = [tile([P, wide[c]], U8, f"u_scales{c}") for c in range(CHUNKS)]
        q_words = tile([P, NQ, PACK], BF16, "q_words")
        q_codes = tile([P, NQ], U32, "q_codes")
        q_scales = tile([P, NQ], U8, "q_scales")
        acc = [psum.tile([NQ, wide[c]], F32, name=f"acc{c}") for c in range(CHUNKS)]
        y = tile([NQ, N], F32, "y")

        def listed(first, last):
            return offsets[:, first // LIST_ROWS : last // LIST_ROWS]

        def chunk(c):
            return listed(EDGES[c], EDGES[c + 1])

        def slot_major(planes):
            return planes.rearrange("p t i -> p i t")

        def quantize(codes, scales, words):
            nc.vector.quantize_mx(
                out=codes[:].bitcast(FP8X4), scales=scales[:], in_=words.rearrange("p i t -> p (i t)")
            )

        def product(c):
            quantize(u_codes[c], u_scales[c], u_words[:, cols[c], :])
            nc.tensor.matmul_mx(
                out=acc[c][:],
                lhsT=q_codes[:].bitcast(FP8X4),
                lhsT_scale=q_scales[:],
                rhs=u_codes[c][:].bitcast(FP8X4),
                rhs_scale=u_scales[c][:],
                start=True,
                stop=True,
            )

        def dense_cols(c):
            return slice(EDGES[c] - EDGES[2], EDGES[c + 1] - EDGES[2])

        def subtract_pair(c):
            nc.vector.tensor_tensor(
                u_words[:, cols[c], 2:4], slot_major(k_high[:, :, cols[c]]), slot_major(r_pairs[:, :, cols[c]]), SUB
            )

        def subtract_dense(c):
            nc.vector.tensor_tensor(u_dense[:, 1, dense_cols(c)], k_high[:, 1, cols[c]], r_last[c][:], SUB)

        def place(c):
            nc.scalar.copy(u_words[:, cols[c], 2:4], slot_major(u_dense[:, :, dense_cols(c)]))

        def scatter_on_vector(first, last):
            nc.vector.tensor_tensor(
                maps[1][:].indirect(listed(first, last)), y[:, first:last], cleared[:, 0 : last - first], ADD
            )

        for t, got in ((0, k_low), (2, k_high)):
            nc.vector.tensor_copy(got[:, 0, :], k_win[:, t, :].indirect(offsets[:]))
            nc.scalar.activation(got[:, 1, :], k_win[:, t + 1, :].indirect(offsets[:]), COPY)
        nc.vector.tensor_copy(r_low[:, 0, :], r_head[:, 0, :].indirect(offsets[:]))
        nc.scalar.activation(r_low[:, 1, :], r_head[:, 1, :].indirect(offsets[:]), COPY)
        nc.vector.tensor_tensor(u_words[:, :, 0:2], slot_major(k_low[:]), slot_major(r_low[:]), SUB)
        nc.scalar.activation(r_mid[:], r_win2[:].indirect(listed(EDGES[2], N)), COPY)
        nc.scalar.activation(r_pairs[:, 0, :], r_win2[:].indirect(listed(0, EDGES[2])), COPY)
        nc.vector.tensor_tensor(u_dense[:, 0, :], k_high[:, 0, EDGES[2] : EDGES[4]], r_mid[:, 0 : 2 * CHUNK], SUB)
        nc.vector.tensor_tensor(u_words[:, cols[4], 2], k_high[:, 0, cols[4]], r_mid[:, dense_cols(4)], SUB)

        nc.vector.tensor_copy(r_last[2][:], r_win3[:].indirect(chunk(2)))
        nc.vector.tensor_copy(r_pairs[:, 1, cols[1]], r_win3[:].indirect(chunk(1)))
        nc.scalar.activation(r_pairs[:, 1, cols[0]], r_win3[:].indirect(chunk(0)), COPY)
        nc.scalar.activation(r_last[3][:], r_win3[:].indirect(chunk(3)), COPY)
        nc.scalar.copy(
            q_words[:].rearrange("p (c i) t -> p c t i", i=4), q_raw[:].rearrange("p t (c i) -> p c t i", i=4)
        )
        subtract_dense(2)
        subtract_pair(0)
        subtract_dense(3)
        subtract_pair(1)
        place(2)
        nc.scalar.activation(r_last4[:], r_win3[:].indirect(chunk(4)), COPY)
        place(3)
        quantize(q_codes, q_scales, q_words[:])
        for c in range(3):
            product(c)
        nc.vector.tensor_tensor(u_words[:, cols[4], 3], k_high[:, 1, cols[4]], r_last4[:], SUB)
        for c in (3, 4):
            product(c)
        nc.scalar.activation(y[:, cols[0]], acc[0][:], COPY, scale=ow_col)
        for c in (1, 2):
            nc.scalar.copy(y[:, cols[c]], acc[c][:])
        scatter_on_vector(0, EDGES[1])
        nc.scalar.activation(
            maps[0][:].indirect(listed(EDGES[1], EDGES[3])), y[:, EDGES[1] : EDGES[3]], COPY, scale=ow_col
        )
        for c in (3, 4):
            nc.vector.tensor_scalar_mul(y[:, cols[c]], acc[c][:], ow_col)
        scatter_on_vector(EDGES[3], N)

        for n, width in enumerate(PIECES):
            first = sum(PIECES[:n])
            piece = slice(first, first + width)
            both = tile([P, width], F32, f"both{first}")
            nc.vector.tensor_tensor(both[:], maps[0][:, piece], maps[1][:, piece], ADD)
            nc.sync.dma_start(out[0][:, piece], both[:])
